import numpy as np, ml_dtypes
CORES = [3,7,11,15,131,135,139,143]
N = 8
BF = ml_dtypes.bfloat16
V, T, BACK, HOPS = 1664, 256, 0, (1, 2, 3, 2, 1)
def wanted(rng, pm, n, share, e):
    u = rng.random((N, 8, 16, n)); v = np.where(rng.random((N, 8, 16, n)) < share, V * u ** e, V * u).astype(np.int64)
    return pm[np.arange(8)[:, None, None], np.minimum(v, V - 1)]
def parts(rng, share=0.3, e=4.0):
    pm = np.argsort(rng.random((8, V)), axis=-1)
    return (rng.integers(0, 16, (N, 8, 16, V)), rng.integers(0, 16, (N, 8, 16, V)), wanted(rng, pm, V, share, e),
            rng.integers(0, 16, (N, 8, 16, T)), wanted(rng, pm, T, share, e), rng.integers(10, 45, (N, 8, 1)), pm)
def worst(x):
    return np.where(x < 8, 15, 0)
def apart(x, d):
    c = x.copy(); left = d.copy()
    for i in range(16):
        up = 15 - x[i] >= x[i]; m = np.minimum(left, np.where(up, 15 - x[i], x[i]))
        c[i] = np.where(up, x[i] + m, x[i] - m); left = left - m
    return c
def pack(x, y, ap, c, al, th):
    def b(a): return np.ascontiguousarray(a.reshape(N, 128, -1)).astype(np.float32).astype(BF)
    def w(a): return np.ascontiguousarray(a.reshape(N, 128, -1)).astype(np.int32)
    return {"fx": b(x), "hx": b(y), "ha": w(ap), "vx": b(c), "va": w(al), "th": th.astype(np.int32)}
def setup_inputs(rng):
    x, y, ap, c, al, th, pm = parts(rng)
    return pack(x, y, ap, c, al, th)
def setup_inputs_ties(rng):
    x, y, ap, c, al, th, pm = parts(rng, 0.5, 6.0); s = rng.integers(1, 4, (1, 8, 1, 1))
    x = (x & 1) * s; y = (y & 1) * s; c = (c & 1) * s; th = s[:, :, 0] * rng.integers(0, 5, (N, 8, 1))
    i = rng.integers(0, T // 2, T); c[:, ::2] = c[:, ::2][..., i]; al[:, ::2] = al[:, ::2][..., i]
    ap[:, :, 8:] = ap[:, :, :8]; al[:, 1::2, 8:] = al[:, 1::2, :8]
    return pack(x, y, ap, c, al, th)
def setup_inputs_crowd(rng):
    x, y, ap, c, al, th, pm = parts(rng)
    n = rng.permutation(np.array([1, 2, 3, 7, 16, 64, 256, V // 2]))
    for g in range(8):
        q = pm[g, :n[g]]
        y[:, g][:, :, q] = worst(x[:, g][:, :, q])
        ap[:, g] = q[rng.integers(0, n[g], (N, 16, V))]; al[:, g] = q[rng.integers(0, n[g], (N, 16, T))]
    i = rng.integers(0, T // 4, T); j = int(np.argmin(n)); c[:, ::2] = c[:, ::2][..., i]; c[:, j] = c[:, j][..., rng.permutation(i)]
    return pack(x, y, ap, c, al, rng.integers(0, 12, (N, 8, 1)))
def setup_inputs_ends(rng):
    x, y, ap, c, al, th, pm = parts(rng); o = rng.permutation(8); h = V // 2
    g = o[0]
    ap[:, g] = rng.integers(0, 2, (N, 16, V)) * (V - 1); al[:, g] = rng.integers(0, 2, (N, 16, T)) * (V - 1)
    y[:, g][:, :, [0, V - 1]] = worst(x[:, g][:, :, [0, V - 1]]); th[:, g] = rng.integers(0, 6, (N, 1))
    g = o[1]
    p = rng.integers(0, 2, (16, 1)) * 15; x[:, g] = p; y[:, g] = 15 - p; c[:, g] = p; th[:, g] = 240
    g = o[2]
    for q in range(N):
        f = rng.permutation(V)[:T]; d = rng.integers(60, 101, T); more = rng.permutation(np.arange(T) & 1)
        y[q, g][:, f] = apart(x[q, g][:, f], d); c[q, g] = apart(x[q, g][:, f], d - th[q, g, 0] - more); al[q, g] = f[None, :]
    g = o[3]
    p = rng.integers(0, 2, (16, 1)) * 15; x[:, g] = p; y[:, g] = 15 - p; c[:, g] = p; th[:, g] = 239
    g = o[4]
    x[:, g] = np.where(rng.random((N, 16, V)) < 0.5, 0, x[:, g]); y[:, g] = x[:, g]; y[:, g][:, :, :h] = worst(x[:, g][:, :, :h]); th[:, g] = rng.integers(0, 20, (N, 1))
    for a, n in ((ap, V), (al, T)):
        a[:, g] = rng.integers(h, V, (N, 16, n)); m = rng.random((N, n)) < 0.5; v = rng.integers(0, h, (N, n))
        a[:, g, 0] = np.where(m, v, a[:, g, 0]); a[:, g, 15] = np.where(m, a[:, g, 15], v)
    g = o[5]
    ap[:, g] = ap[:, g, :1]; al[:, g] = al[:, g, :1]
    g = o[6]
    y[:, g] = x[:, g]; th[:, g] = 0
    for q in range(N):
        f = rng.integers(0, V, T); m = rng.random(T) < 0.75
        al[q, g] = f[None, :]; c[q, g] = np.where(m[None, :], x[q, g][:, f], c[q, g])
    g = o[7]
    y[:, g] = x[:, g]; th[:, g] = rng.integers(0, 16, (N, 1)); R = len(HOPS); S = [sum(HOPS[:j]) for j in range(R)]
    o7 = rng.permutation(V); rest = o7[N + N * R:]
    ap[:, g] = rest[rng.integers(0, len(rest), (N, 16, V))]; al[:, g] = rest[rng.integers(0, len(rest), (N, 16, T))]
    for q in range(N):
        a = o7[q]; y[q, g][:, [a]] = apart(x[q, g][:, [a]], np.array([120]))
        for j in range(R):
            s = (q - S[j]) % N; t = q * R + j; home = apart(x[q, g][:, [a]], np.array([104 - 16 * j]))[:, 0]
            way = [(s + S[i]) % N for i in range(j)]; seen = [i for i in range(j) if way[i] == q]
            if not seen:
                c[s, g, :, t] = home; al[s, g, :, t] = a
            else:
                w = [way[m] for m in range(seen[-1] + 1, j) if way[m] not in way[:m]][0]; b = o7[N + t]
                x[w, g, :, b] = worst(home); y[w, g, :, b] = home; ap[w, g, :, b] = a
                c[s, g, :, t] = x[w, g, :, b]; al[s, g, :, t] = b
    return pack(x, y, ap, c, al, th)
def setup_inputs_full(rng):
    x, y, ap, c, al, th, pm = parts(rng); y = x.copy(); th = rng.integers(0, 60, (N, 8, 1)); z = rng.integers(0, 2, 8); q0 = int(rng.integers(0, N))
    for q in range(N):
        kinds = rng.permutation(np.array([0, 0, 1, 2, 3, 3, 4, 4]))
        for g in range(8):
            e = int(z[g] + q) % 2; kind = 0 if q == q0 else int(kinds[g])
            y[q, g][:, e::2] = worst(x[q, g][:, e::2]); far = e + 2 * rng.permutation(V // 2)
            f = far[:T]; d = rng.integers(0, 60, T)
            if kind == 1:
                n = min(T, V // 16); r = e + 2 * int(rng.integers(0, 8)); f = rng.permutation((r + 16 * rng.permutation(V // 16)[:n])[np.arange(T) % n])
            if kind == 2:
                f = e + 2 * (rng.permutation(T) + int(rng.integers(0, 2)) * (V // 2 - T))
            if kind == 3:
                tt = np.sort(rng.permutation(T).reshape(-1, 2), axis=1); f = np.zeros(T, np.int64); f[tt] = far[:T // 2][:, None]; d[tt] = rng.integers(0, 30, tt.shape) + np.array([30, 0])
            if kind == 4:
                a = far[0]; x[q, g, :, a] = 15 * rng.integers(0, 2, 16); y[q, g, :, a] = 15 - x[q, g, :, a]; th[q, g] = 0
                f = np.full(T, a); d = np.maximum(min(T, 240) - 1 - np.arange(T), 0)
            c[q, g] = apart(x[q, g][:, f], d); al[q, g] = f[None, :]
    return pack(x, y, ap, travel(c, -HOPS[0]), travel(al, -HOPS[0]), th)
def setup_inputs_spread(rng):
    x, y, ap, c, al, th, pm = parts(rng)
    def f(n): return np.minimum((np.exp2(4 * rng.random((N, 8, 1, n))) * rng.random((N, 8, 16, n)) + 0.5).astype(np.int64), 15)
    x = f(V); y = f(V); c = f(T); y = np.where(rng.random((N, 8, 1, V)) < 0.1, worst(x), y)
    ap = wanted(rng, pm, V, 0.8, np.exp2(4 * rng.random((N, 8, 1, V)))); al = wanted(rng, pm, T, 0.8, np.exp2(4 * rng.random((N, 8, 1, T))))
    th = (120 * rng.random((N, 8, 1)) ** 3).astype(np.int64); th[:, rng.integers(0, 8)] = 0
    return pack(x, y, ap, c, al, th)
def check_inputs(d):
    bad = []
    for k in ("fx", "hx", "vx"):
        v = np.asarray(d[k]).astype(np.float64)
        if not np.all((v >= 0) & (v <= 15) & (v == np.floor(v))): bad.append("whole numbers of " + k)
    for k, hi in (("ha", V - 1), ("va", V - 1), ("th", 240)):
        if np.min(d[k]) < 0 or np.max(d[k]) > hi: bad.append("range of " + k)
    return bad
def travel(a, h):
    b = np.roll(a, h, axis=0)
    if BACK: b[..., T - BACK:] = np.roll(a[..., T - BACK:], -h, axis=0)
    return b
def reference(fx, hx, ha, vx, va, th):
    x = fx.astype(np.float32).astype(np.int32).reshape(N, 8, 16, V)
    y = hx.astype(np.float32).astype(np.int32).reshape(N, 8, 16, V)
    ap = ha.astype(np.int64).reshape(N, 8, 16, V)
    hid = np.zeros((N, 8, V), np.int64) + np.arange(N)[:, None, None] * V + np.arange(V)
    c = vx.astype(np.float32).astype(np.int32).reshape(N, 8, 16, T)
    al = va.astype(np.int64).reshape(N, 8, 16, T)
    tid = np.zeros((N, 8, T), np.int64) + N * V + np.arange(N)[:, None, None] * T + np.arange(T)
    length = np.zeros((N, 8, T), np.int64); lim = th.astype(np.int64)
    ri = np.arange(N)[:, None, None]; gi = np.arange(8)[None, :, None]
    for h in HOPS:
        own = np.add.reduce(np.abs(x - y), axis=2)
        xa = np.take_along_axis(x, al.reshape(N, 8, 1, 16 * T), 3).reshape(N, 8, 16, 16, T)
        there = np.add.reduce(np.abs(xa - c[:, :, :, None, :]), axis=2)
        gain = np.take_along_axis(own, al.reshape(N, 8, 16 * T), 2).reshape(N, 8, 16, T).astype(np.int64) - there
        k = np.argmax(gain, axis=2)[:, :, None]
        best = np.take_along_axis(gain, k, 2)[:, :, 0]; fam = np.take_along_axis(al, k, 2)[:, :, 0]
        offer = best > lim
        key = np.where(offer, best * T + (T - 1 - np.arange(T)), -1)
        top = np.full((N, 8, V), -1, np.int64); np.maximum.at(top, (ri, gi, fam), key)
        n_, g_, t_ = np.nonzero(offer & (np.take_along_axis(top, fam, 2) == key)); f_ = fam[n_, g_, t_]
        old = y[n_, g_, :, f_]; y[n_, g_, :, f_] = c[n_, g_, :, t_]; c[n_, g_, :, t_] = old
        old = ap[n_, g_, :, f_]; ap[n_, g_, :, f_] = al[n_, g_, :, t_]; al[n_, g_, :, t_] = old
        old = hid[n_, g_, f_]; hid[n_, g_, f_] = tid[n_, g_, t_]; tid[n_, g_, t_] = old
        length[n_, g_, t_] += 1
        c = travel(c, h); al = travel(al, h); tid = travel(tid, h); length = travel(length, h)
    return {"yh": hid.astype(np.float32), "yt": tid.astype(np.float32), "yl": length.astype(np.float32)}

@@ -1,0 +1,413 @@
+from concourse.mybir import AluOpType, AxisListType, ActivationFunctionType
+
+V, TK, HOPS = 1664, 256, (1, 2, 3, 2, 1)
+R = len(HOPS)
+MID = 1472
+
+_B = {
+    "bfloat16": dict(xs=V, Pf=V + TK * R, mn=V, CS=TK * 4, m=16 * TK, ug=16 * TK, A=(16, 16), L=256, R2=512, junk=2048, I=128,
+                     Wm=16, Wc=256, Wu=(16, 16), Wy=(8, 16), Wn=(8, 16), HL=512, Ws=128, VV=16, Rep=128, WB=256, C4=4 * TK),
+    "float16": dict(XR=TK * R, XS=TK * 4, Y=TK, Rb=128, P4=512, Z=240),
+    "int32": dict(Pl=V + TK * 4, Vi=16, D6=(16, 6), pt=16, pi=8, pj=8, pk=16, p8=8, th1=8, th2=8),
+    "uint16": dict(O=TK, ix=16, fi=16, ob=8, op=2),
+    "float32": dict(U=V + TK * R, GS=TK * R, SC=256, C6=(16, 6), t1=16, t2=16, po=16, r=16, yy=16, yc=16, D1=256, Ag=256,
+                    B=256, Gt=256, F1=32, F2=32, FR=32, pf=8, PD=128, G8=256, G16=256, mk=256, Wt=(16, 16), Wv=(16, 16),
+                    mk3=(16, 16), CC=24, CD=16, Sh=128, THV=16, base=16 * R, rs=128, D0=256),
+}
+SCRATCH = {k: ("sbuf", [128] + (list(s) if isinstance(s, tuple) else [s]), d) for d, bufs in _B.items() for k, s in bufs.items()}
+SCRATCH.update({"ps%d" % b: ("psum", [128, 512], "float32") for b in range(8)})
+SEMAPHORES = (["sv", "sa", "st", "sg", "sent", "lva", "lvx", "lth", "lha", "o1", "o2", "o3", "arF", "rep"]
+              + ["l%s%d" % (s, i) for s in "fh" for i in range(4)] + ["ar%s%d" % (s, i) for s in "XcD" for i in range(1, R)])
+
+ALU = AluOpType
+ACT = ActivationFunctionType
+ADD, SUB, MUL, MAX, MIN, EQ = ALU.add, ALU.subtract, ALU.mult, ALU.max, ALU.min, ALU.is_equal
+SHR, AND = ALU.arith_shift_right, ALU.bitwise_and
+RU, RPH, RPL, RFH, RFL, RONE, RID, RLEN = range(8)
+(cK1, cK2, cA, cIS, cCC, cB0, cE1, cHID, cML, cBL, cSR, cBR, cKEEP, cD1, cM10, cM15) = range(16)
+BANKS = ["b%d" % b for b in range(8)]
+PV = [(k, k + 1) for k in range(7)] + [(7, 11), (11, 14), (14, 15), (15, 16)]
+PA = [(0, 4), (4, 7), (7, 11), (11, 14), (14, 15), (15, 16)]
+
+
+def rank_program(g, core, T, topo):
+    rank = T.rank_of(core)
+    if rank is None:
+        return
+    n = len(T.cores)
+    v, a, t = g.vector, g.scalar, g.tensor
+    Q = {"v": v, "a": a, "t": t, "g": g, "s": g.sync}
+    cnt = {"v": 0, "a": 0, "t": 0, "g": 0}
+    seen = {e: {} for e in Q}
+    lastw, readers, final, sent = {}, {}, {}, [0]
+    ps = [T["ps%d" % b] for b in range(8)]
+
+    def wait(e, tok):
+        if seen[e].get(tok[0], 0) < tok[1]:
+            Q[e].wait_ge(T.sem[tok[0]], tok[1])
+            seen[e][tok[0]] = tok[1]
+            for s, c in tok[3].items():
+                seen[e][s] = max(seen[e].get(s, 0), c)
+
+    def deps(e, r, w):
+        toks = [lastw[k] for k in r if k in lastw]
+        for k in w:
+            part = k.endswith("+")
+            k = k.rstrip("+")
+            own = part or k in BANKS
+            if k in lastw and not (own and lastw[k][2] == e):
+                toks.append(lastw[k])
+            toks += readers.get(k, [])
+        for tok in sorted(toks, key=lambda x: -x[1]):
+            wait(e, tok)
+
+    def note(tok, r, w):
+        for k in r:
+            readers.setdefault(k, []).append(tok)
+        for k in w:
+            lastw[k.rstrip("+")] = tok
+            readers[k.rstrip("+")] = []
+
+    def op(e, fn, r, w):
+        r, w = r.split(), w.split()
+        deps(e, r, w)
+        cnt[e] += 1
+        fn().then_inc(T.sem["s" + e], 1)
+        note(("s" + e, cnt[e], e, dict(seen[e])), r, w)
+
+    def dma(e, sem, pairs, r, w):
+        r, w = r.split(), w.split()
+        deps(e, r, w)
+        for out, in_ in pairs:
+            Q[e].dma_start(out, in_).then_inc(T.sem[sem], 16)
+            final[sem] = final.get(sem, 0) + 16
+        note((sem, final[sem], "dma", dict(seen[e])), r, w)
+
+    def send(dst, sem, out, in_, r):
+        deps("g", [r], ())
+        rid, pid = topo.addr(dst, core)
+        g.remote_dma(out, in_, T.sem[sem], T.sem.sent, pid, rid, topo.mask(core, dst))
+        sent[0] += len(topo.engines(core, dst))
+
+    def ts(out, in0, s1, o0, r, w, s2=None, o1=None):
+        if o1 is None:
+            op("v", lambda: v.tensor_scalar(out, in0, s1, None, o0), r, w)
+        else:
+            op("v", lambda: v.tensor_scalar(out, in0, s1, s2, o0, o1), r, w)
+
+    def tt(out, in0, in1, o, r, w):
+        op("v", lambda: v.tensor_tensor(out, in0, in1, o), r, w)
+
+    def cp(out, in_, r, w):
+        op("v", lambda: v.tensor_copy(out, in_), r, w)
+
+    def tr(out, in_, r, w):
+        op("v", lambda: v.transpose(out, in_), r, w)
+
+    def ms(ap, c, w):
+        op("v", lambda: v.memset(ap, c), "", w)
+
+    def act(out, in_, r, w, func=ACT.Identity, **kw):
+        op("a", lambda: a.activation(out, in_, func, **kw), r, w)
+
+    def mm(out, lhsT, rhs, start, stop, r, x):
+        op("t", lambda: t.matmul(out, lhsT, rhs, start, stop), r, x)
+
+    def iota(out, pat, base, cm, w):
+        op("g", lambda: g.iota(out, pat, base, cm, allow_small_or_imprecise_dtypes=True), "", w)
+
+    def iint(out, pat, base, cm, w):
+        op("g", lambda: g.iota(out, pat, base, cm), "", w)
+
+    def col(c):
+        return T.CC[:, c:c + 1]
+
+    def names(p, lo, hi):
+        return " " + " ".join("%s%d" % (p, j) for j in range(lo, hi)) + " "
+
+    def sel(c0, c1, row, val, step=0, cmp="eq"):
+        ap, ks = T.VV[0:16, c0:c1 + 1], names("V", c0, c1 + 1)
+        o, b, cm = {"eq": (ALU.not_equal, -row, 1), "lt": (ALU.is_ge, -row, 1), "ge": (ALU.is_gt, row, -1)}[cmp]
+        op("g", lambda: g.affine_select(ap, ap, [[step, c1 + 1 - c0]], o, float(val), b, cm), ks, ks)
+
+    for i in range(R):
+        e_in = len(topo.engines(T.cores[(rank - HOPS[i]) % n], core))
+        for k in (["X%d" % (i + 1), "c%d" % (i + 1), "D%d" % (i + 1)] if i + 1 < R else ["F"]):
+            lastw[k] = ("ar" + k, e_in, "far", {})
+
+    CH = [(0, 512), (512, 1024), (1024, 1536), (1536, V)]
+    dma("s", "lva", [(T.Pl[:, V:V + TK], T.va[:])], "", "l0")
+    for i, (lo, hi) in enumerate(CH):
+        dma("a", "lh%d" % i, [(T.Pf[:, lo:hi], T.hx[:, lo:hi])], "", "h%d" % i)
+        dma("s", "lf%d" % i, [(T.xs[:, lo:hi], T.fx[:, lo:hi])], "", "f%d" % i)
+    dma("s", "lvx", [(T.Pf[:, V:V + TK], T.vx[:])], "", "c0")
+    dma("s", "lth", [(T.th1[0:1, 0:8], T.th[:])], "", "th1")
+    FX, HX = names("f", 0, 4), names("h", 0, 4)
+
+    ms(T.VV[0:16, :], 0.0, names("V", 0, 16))
+    ms(T.HL[0:64, :], 0.0, "HL")
+    iint(T.pi[:, 0:1], [[0, 1]], 0, 1, "pi")
+    iota(T.PD[:, :], [[1, 128]], 0, -1, "PD")
+    iota(T.G8[:, :], [[0, 32], [1, 8]], 0, 0, "G8")
+    iota(T.Gt[0:16, 0:128], [[0, 8], [1, 16]], 0, -1, "Gt")
+    sel(cK1, cK2, RU, 65536)
+    sel(cA, cA, RPH, 1)
+    sel(cIS, cB0, RONE, 1)
+    sel(cK1, cK2, RFH, 128, step=RFH - RPH)
+    sel(cA, cA, RFH, 1)
+    sel(cCC, cB0, RLEN, 1024)
+    sel(cK1, cK2, RFL, 1, step=RFL - RPL)
+    sel(cA, cA, RID, 128)
+    sel(cCC, cCC, RID, V * rank)
+    iota(T.G16[:, :], [[0, 2], [1, 8], [0, 16]], 0, 0, "G16")
+    iota(T.Wt[:], [[-4096, 16], [0, 16]], 61440, 0, "Wt")
+    iota(T.mk3[:], [[0, 32], [1, 8]], 0, 0, "mk3")
+    for j in range(4):
+        act(T.HL[0:1, 128 * j:128 * j + 128], T.PD[0:1, :], "PD HL", "HA+")
+        if j:
+            act(T.HL[32:33, 128 * j:128 * j + 128], T.PD[32:33, :], "PD HL", "HA+", scale=0.0, bias=float(j))
+
+    ms(T.Ws[0:64, :], 0.0, "Ws")
+    ms(T.Wy[:], 0.0, "Wy")
+    ms(T.Wn[:], 0.0, "Wn")
+    for row in (RPL, RFL, RID):
+        ms(T.Ws[0:1, row::16], 1.0, "Ws" if row == RPL else "Ws+")
+    for row, val in ((RPH, 1.0), (RFH, 1.0), (RID, 128.0)):
+        ms(T.Ws[32:33, row::16], val, "Ws+")
+    ts(T.pj[:, 0:1], T.pi[:, 0:1], 4, SHR, "pi", "pj0")
+    ts(T.pj[:, 1:2], T.pi[:, 0:1], 4, SHR, "pi", "pj1", 1, AND)
+    ts(T.I[:, :], T.PD[:, :], 0.0, EQ, "PD", "I")
+    cp(T.pf[:, 0:2], T.pj[:, 0:2], "pj0 pj1", "pf")
+    ts(T.pf[:, 2:3], T.pf[:, 1:2], 0.0, EQ, "pf", "pe")
+    par = [T.pf[:, 2:3], T.pf[:, 1:2]]
+    for e in (1, 0):
+        for gp in range(2):
+            j = 2 * e + gp
+            ts(T.P4[:, 128 * j:128 * j + 128], T.PD[:, :], float(16 * (gp - e)), EQ, "PD pf" if e else "PD pe", "P4+", par[e], MUL)
+    ts(T.mk[:, :], T.G8[:, :], T.pf[:, 0:1], EQ, "G8 pf", "mk")
+    ts(T.Rep[0:16, :], T.Gt[0:16, 0:128], 0.0, EQ, "Gt", "Rep")
+    cp(T.Wy[:, :, RU], T.mk[:, 0:8], "mk", "Wy")
+    ts(T.Wn[:, :, RU], T.mk[:, 0:8], -2.0, MUL, "mk", "Wn")
+    cp(T.XR[:, 0:TK], T.Pl[:, V:V + TK], "l0", "X0")
+    mm(ps[3][:, 0:5], T.Rep[0:16, :], T.VV[0:16, 0:5], True, True, "Rep" + names("V", 0, 5), "b3")
+    act(T.CC[:, 0:5], ps[3][:, 0:5], "", "CC0 b3")
+    for i in range(4):
+        act(T.CD[:, i:i + 1], col(cA), "CC0", "CD%d" % i, scale=float(4 * i), bias=col(cCC))
+
+    def turn_lists(i):
+        for h in range(2):
+            tr(T.Y[:, h::2], T.XR[:, TK * i + 128 * h:TK * i + 128 * h + 128], "X%d" % i, "Y%d" % h)
+        for b in range(4):
+            for e in range(2):
+                for gp in range(2):
+                    j = 2 * e + gp
+                    mm(ps[2][:, 2 * b + e:256:8], T.P4[:, 128 * j:128 * j + 128],
+                       T.Y[:, 64 * b + 32 * gp:64 * b + 32 * gp + 32], gp == 0, gp == 1, "P4 Y0 Y1", "b2")
+        if 0 < i < R - 1:
+            cp(T.Pl[:, V + TK * i:V + TK * (i + 1)], T.XR[:, TK * i:TK * (i + 1)], "X%d" % i, "l%d" % i)
+        cp(T.O[:, :], ps[2][:, 0:256], "", "O b2")
+
+    turn_lists(0)
+
+    def homes(i):
+        mm(ps[i % 2][:, 0:CH[i][1] - CH[i][0]], T.I[:, :], T.Pf[:, CH[i][0]:CH[i][1]], True, True, "I h%d" % i, "b%d" % (i % 2))
+
+    homes(0)
+    homes(1)
+    for i, (lo, hi) in enumerate(CH):
+        tt(T.mn[:, lo:hi], T.xs[:, lo:hi], ps[i % 2][:, 0:hi - lo], MIN, "f%d" % i, "mn%d b%d" % (i, i % 2))
+        o, bk = ps[4 + i][:, 0:hi - lo], "b%d" % (4 + i)
+        mm(o, T.Ws[0:64, :], T.HL[0:64, 0:hi - lo], True, False, "Ws HL HA", bk)
+        mm(o, T.Wy[:], T.Pf[:, lo:hi], False, False, "Wy h%d" % i, bk)
+        if i < 2:
+            homes(i + 2)
+        mm(o, T.Wn[:], T.mn[:, lo:hi], False, True, "Wn mn%d" % i, bk)
+        act(T.U[:, lo:hi], o, "CD%d" % i, "U+ " + bk, bias=T.CD[:, i:i + 1])
+    ts(T.Wm[:, :], T.mk[:, 0:16], 131072.0, MUL, "mk", "Wm")
+    ts(T.Wc[:, :], T.G16[:, :], T.pf[:, 0:1], EQ, "G16 pf", "Wc", -65536.0, MUL)
+    ts(T.mk3[:], T.mk3[:], T.pf[:, 0:1], EQ, "mk3 pf", "mk3")
+    for K in range(2):
+        ts(T.Wv[:, :, 8 * K:8 * K + 8], T.Wt[:, :, 8 * K:8 * K + 8], col(cIS), MUL, "Wt CC0", "Wv+", col(cK1 + K), ADD)
+
+    sel(cB0, cB0, RPH, 13)
+    sel(cE1, cE1, RPH, 1)
+    sel(cHID, cHID, RID, 1)
+    sel(cML, cML, 6, 1, cmp="ge")
+    sel(cBL, cBL, 6, 1, cmp="lt")
+    sel(cSR, cSR, 10, 2.0 ** 29, cmp="lt")
+    sel(cBR, cBR, 10, -2.0 ** 20, cmp="ge")
+    sel(cKEEP, cKEEP, RU, 1)
+    sel(cD1, cD1, 0, 2.0 ** 20, cmp="ge")
+    sel(cM10, cM15, 10, -1, step=-5)
+    sel(cB0, cB0, RPL, 255)
+    sel(cSR, cSR, 6, 2.0 ** 20, cmp="lt")
+    sel(cBR, cBR, 11, -2.0 ** 28, cmp="ge")
+    sel(cKEEP, cKEEP, RFH, 1)
+    sel(cD1, cD1, RLEN, 1)
+    sel(cSR, cSR, 5, 2.0 ** 12, cmp="lt")
+    sel(cBR, cBR, 15, -2.0 ** 12, cmp="ge")
+    sel(cKEEP, cKEEP, RFL, 1)
+    sel(cSR, cSR, 4, -2.0 ** 28, cmp="lt")
+    iota(T.base[:, :], [[TK, R], [128, 2], [0, 8]], V - MID, 1, "base")
+    iota(T.D0[:, :], [[1, TK]], n * V + rank * TK, 0, "D00")
+    for j in (4, 15):
+        iota(T.A[:, :, j], [[-128, 2], [0, 8]], 255, -1, "Att+")
+    iint(T.pk[:, :], [[-1, 16]], 16, 1, "pk")
+    iint(T.p8[:, :], [[1, 8]], 0, 0, "p8")
+    op("g", lambda: g.partition_broadcast(T.th2[:, :], T.th1[0:1, :], 128), "th1 p8", "th2")
+
+    def late_constants():
+        mm(ps[3][:, 8:19], T.Rep[0:16, :], T.VV[0:16, 5:16], True, True, "Rep" + names("V", 5, 16), "b3")
+        act(T.CC[:, 5:16], ps[3][:, 8:19], "", "CC1 b3")
+        for e in range(2):
+            act(T.CC[:, 16 + 2 * e:18 + 2 * e], T.CC[:, cSR:cBR + 1], "CC1 pf pe", "CR+", scale=par[e])
+        act(T.U[:, V:V + TK], T.D0[:, :], "D00 CC1", "D0", scale=col(cHID))
+        for i in range(R):
+            act(T.CD[:, 4 + i:5 + i], col(cE1), "CC1", "CB+", scale=float(2 * i), bias=col(cB0))
+        ms(T.rs[:, :], 0.0, "rs")
+        ms(T.C6[:], 3.5, "C6")
+        ts(T.Z[:, :], T.G8[:, 0:240], 0.0, MUL, "G8", "Z")
+        ts(T.pk[:, :], T.pk[:, :], 15, AND, "pk", "pk")
+        ms(T.rs[:, 0::16], -2.0 ** 26, "rs")
+        ms(T.C6[:, :, 0::5], 0.0, "C6")
+        for h in range(2):
+            ts(T.THV[:, 8 * h:8 * h + 8], T.th2[:, :], 1.0, ADD, "th2", "THV+", 65536.0, MUL)
+        ts(T.pj[:, 3:4], T.pi[:, 0:1], 8, AND, "pi", "q3")
+        ts(T.pj[:, 4:5], T.pi[:, 0:1], 14, AND, "pi", "q4")
+        ts(T.pj[:, 5:6], T.pi[:, 0:1], 1, AND, "pi", "q5")
+        ts(T.Z[:, 112:128], T.pk[:, :], 0.0, EQ, "pk", "Z")
+        cp(T.pf[:, 3:6], T.pj[:, 3:6], "q3 q4 q5", "pq")
+        ts(T.p8[:, :], T.p8[:, :], T.pf[:, 3:4], ADD, "p8 pq th2", "p8")
+        ts(T.pf[:, 6:7], T.pf[:, 4:5], 16.0, MUL, "pq", "pq6", T.pf[:, 5:6], ADD)
+        cp(T.ob[:, :], T.p8[:, :], "p8", "ob")
+
+    def last_constants():
+        ts(T.WB[:, 0:128], T.PD[:, :], float(RU - 10), EQ, "PD CC1", "WB+", col(cM10), MUL)
+        ts(T.WB[:, 128:256], T.PD[:, :], float(RPL - 15), EQ, "PD CC1", "WB+", col(cM15), MUL)
+        ts(T.Sh[:, :], T.PD[:, :], 0.0, EQ, "PD CC1", "Sh", col(cHID), MUL)
+        for gp in range(2):
+            ts(T.op[:, gp:gp + 1], T.pf[:, 6:7], float(RID + 16 * gp), ADD, "pq6", "op+")
+
+    def scans(K):
+        for h in range(2):
+            op("v", lambda: v.tensor_tensor_scan(T.SC[:, 128 * h:128 * h + 128], T.rs[:, :], ps[h][:, 128 * K:128 * K + 128],
+                                                 0.0, ADD, MAX), "rs", "SC%d b%d" % (h, h))
+
+    def payload():
+        tt(T.t1[:, :], T.THV[:, :], T.SC[:, 15::16], SUB, "THV SC0 SC1", "t1")
+        ts(T.pt[:, :], T.Vi[:, :], 4095, AND, "Vi", "pt")
+        ts(T.t2[:, :], T.t1[:, :], 0.0, MAX, "t1", "t2", float(-MID), ADD)
+        tt(T.po[:, :], T.t2[:, :], T.pt[:, :], ADD, "t2 pt", "po")
+
+    def offsets(i, out, key, b, meanwhile=None):
+        tt(T.yy[:, :], T.r[:, :], T.po[:, :], ADD, "rv ra po", "yy")
+        tt(T.yc[:, :], T.yy[:, :], T.base[:, 16 * i:16 * i + 16], MIN, "yy base", "yc")
+        tt(T.Rb[:, :], T.yc[:, :].indirect(T.ob[:, :]), T.mk[:, 0:128], MUL, "yc ob mk", "Rb")
+        for gg in range(8):
+            mm(ps[b][:, 0:16], T.Z[:, 112 - 16 * gg:240 - 16 * gg], T.Rb[:, 16 * gg:16 * gg + 16], gg == 0, gg == 7, "Z Rb", "b%d" % b)
+        if meanwhile:
+            meanwhile()
+        ts(out[:, :], ps[b][:, 0:16], float(MID), ADD, "", "%s b%d" % (key, b))
+
+    for i in range(R):
+        last = i == R - 1
+        dst = T.cores[(rank + HOPS[i]) % n]
+        c0 = V + TK * i
+        mine = slice(TK * i, TK * (i + 1))
+        dma("s", "rep", [(T.C4[:, TK * j:TK * (j + 1)], T.Pf[:, c0:c0 + TK]) for j in range(4)], "c%d" % i, "C4")
+        if i == 0:
+            dma("s", "lha", [(T.Pl[:, 0:V], T.ha[:])], "f3 h3", "Pl")
+        else:
+            turn_lists(i)
+        for h in range(2):
+            mm(ps[h][:, 0:256], T.Pf[:, c0 + 128 * h:c0 + 128 * h + 128], T.Wc[:, :], True, False, "c%d Wc" % i, "b%d" % h)
+        for k1, key, k0 in sorted([(k1, "m", k0) for k0, k1 in PV] + [(k1, "ug", k0) for k0, k1 in PA]):
+            off = T.O[:, 16 * k0:16 * k1]
+            if key == "ug":
+                act(T.ug[:, TK * k0:TK * k1], T.U[:, 0:V].indirect(off), "U O", names("ug", k0, k1), func=ACT.Copy)
+            elif k1 - k0 == 1:
+                tt(T.m[:, TK * k0:TK * k1], T.xs[:, :].indirect(off), T.Pf[:, c0:c0 + TK], MIN, FX + "O c%d" % i, "m%d" % k0)
+            else:
+                tt(T.m[:, TK * k0:TK * k1], T.xs[:, :].indirect(off), T.C4[:, 0:TK * (k1 - k0)], MIN, FX + "O C4", names("m", k0, k1))
+            if i == 0 and k1 == 1:
+                tt(T.Wu[:], T.Wv[:], T.mk3[:], MUL, "Wv mk3", "Wu")
+            for k in range(k0, k1):
+                for h in range(2):
+                    mm(ps[h][:, k:256:16], T[key][:, TK * k + 128 * h:TK * k + 128 * h + 128],
+                       T.Wm[:, :] if key == "m" else T.Wu[:, k, :], False, k == 15 and key == "ug",
+                       "%s%d W%s" % (key, k, key[0]), "b%d" % h)
+        if i == 0:
+            late_constants()
+        act(T.D1[:, :], T.U[:, c0:c0 + TK], "D%d CC1" % i, "Dp", bias=col(cD1))
+        scans(0 if last else 1)
+        cp(T.Vi[:, :], T.SC[:, 15::16], "SC0 SC1", "Vi")
+        for j, sh in enumerate((9, 6, 3)):
+            ts(T.D6[:, :, 1 + j], T.Vi[:, :], sh, SHR, "Vi", "d%d" % (1 + j), 7, AND)
+        ts(T.D6[:, :, 4], T.Vi[:, :], 7, AND, "Vi", "d4")
+        for j in (0, 5):
+            ts(T.D6[:, :, j], T.Vi[:, :], 16, SHR, "Vi", "d%d" % j)
+        tt(T.A[:, :, 5:11], T.D6[:], T.C6[:], SUB, names("d", 0, 6) + "C6", "Ad")
+        for j in (0, 11):
+            tt(T.A[:, :, j:j + 4], T.A[:, :, 6:10], T.A[:, :, 6:10], MUL, "Ad", "As%d" % j)
+        for b in (3, 2):
+            for h in range(2):
+                mm(ps[b][:, 128 * h:128 * h + 128], T.A[:, 8 * h:8 * h + 8, :], T.I[:, :], True, True, "Ad As0 As11 Att I", "b%d" % b)
+        payload()
+        ts(T.R2[:, 0:256], ps[3][:, 0:256], col(16), MUL, "CR", "R0 b3", col(17), ADD)
+        act(T.L[:, 0:128], ps[2][:, 0:128], "CC1", "L0 b2", scale=col(cML), bias=col(cBL))
+        act(T.R2[:, 256:512], ps[2][:, 0:256], "CR", "R1 b2", scale=col(18), bias=col(19))
+        ts(T.L[:, 128:256], ps[3][:, 128:256], col(cML), MUL, "CC1", "L1 b3", col(cBL), ADD)
+        for h in range(2):
+            for q in range(4):
+                bk = "b%d" % (4 + q)
+                mm(ps[4 + q][:, :], T.L[32 * q:32 * q + 32, 128 * h:128 * h + 128], T.R2[32 * q:32 * q + 32, :], True, True,
+                   "L%d R0 R1" % h, bk)
+                for gp in range(2):
+                    s = 8 * h + 2 * q + gp
+                    src = ps[4 + q][:, 256 * gp:256 * gp + 256]
+                    if q % 2 == 1:
+                        op("v", lambda: v.tensor_reduce(T.r[:, s:s + 1], src, AxisListType.X, MAX), "", "rv+ " + bk)
+                    else:
+                        j = TK * (s // 4 * 2 + gp)
+                        act(T.junk[:, j:j + TK], src, "", "ra+ " + bk, func=ACT.Relu, accum_out=T.r[:, s:s + 1])
+        if not last:
+            offsets(i, T.ix, "ix", 2, lambda: scans(0))
+            cp(T.XS[:, mine], T.Pl[:, 0:c0 + TK].indirect(T.ix[:, :]), "ix Pl" + names("l", 0, i + 1), "XS%d" % i)
+            act(T.CS[:, mine], T.Pf[:, 0:c0 + TK].indirect(T.ix[:, :]), "ix" + HX + names("c", 0, i + 1), "CS%d" % i, func=ACT.Copy)
+            send(dst, "arX%d" % (i + 1), T.XR[:, TK * (i + 1):TK * (i + 2)], T.XS[:, mine], "XS%d" % i)
+            send(dst, "arc%d" % (i + 1), T.Pf[:, c0 + TK:c0 + 2 * TK], T.CS[:, mine], "CS%d" % i)
+            cp(T.Vi[:, :], T.SC[:, 15::16], "SC0 SC1", "Vi")
+            payload()
+
+        def new_rows():
+            if i == 0:
+                last_constants()
+            mm(ps[6][:, 0:256], T.WB[:, 0:128], T.L[:, :], True, False, "WB L0 L1", "b6")
+            mm(ps[6][:, 0:256], T.WB[:, 128:256], T.L[:, :], False, False, "WB L0 L1", "b6")
+            mm(ps[6][:, 0:256], T.Sh[:, :], T.U[:, c0:c0 + TK], False, True, "Sh D%d" % i, "b6")
+            act(T.B[:, :], ps[6][:, 0:256], "CB", "B b6", bias=T.CD[:, 4 + i:5 + i])
+
+        if not last:
+            new_rows()
+        offsets(i, T.fi, "fi", 3, new_rows if last else None)
+        olds = names("D", 0, i + 1)
+        win = T.U[:, 0:c0 + TK]
+        act(T.Ag[:, :], win.indirect(T.fi[:, :]), "U fi CC1" + olds, "Ag", scale=col(cKEEP))
+        tt(T.GS[:, mine], win.indirect(T.fi[:, :]), T.D1[:, :], MIN, "U fi Dp" + olds, "G%d" % i)
+        if not last:
+            send(dst, "arD%d" % (i + 1), T.U[:, c0 + TK:c0 + 2 * TK], T.GS[:, mine], "G%d" % i)
+        else:
+            tr(T.Gt[:, :], T.GS[:, mine], "G%d" % i, "Gt")
+            cp(T.F1[:, :], T.Gt[:, :].indirect(T.op[:, :]), "Gt op", "F1")
+            tr(T.F2[:, :], T.F1[:, :], "F1", "F2")
+            send(dst, "arF", T.FR[:, :], T.F2[:, :], "F2")
+        tt(win.indirect(T.fi[:, :]), T.Ag[:, :], T.B[:, :], ADD, "Ag B fi", "U" + olds)
+
+    dma("s", "o1", [(T.yh[:], T.U[RID::16, 0:V])], "U", "")
+    dma("a", "o2", [(T.yt[:], T.FR[0::2, :])], "F", "")
+    dma("s", "o3", [(T.yl[:], T.FR[1::2, :])], "F", "")
+    for e in cnt:
+        wait("g", ("s" + e, cnt[e], e, {}))
+    wait("g", ("sent", sent[0], "g", {}))
+    for s in final:
+        wait("g", (s, final[s], "dma", {}))

@@ -1,33 +1,41 @@
-from concourse.mybir import AluOpType, AxisListType, ActivationFunctionType
+from concourse.mybir import AluOpType, ActivationFunctionType, AxisListType
 
 V, TK, HOPS = 1664, 256, (1, 2, 3, 2, 1)
 R = len(HOPS)
 MID = 1472
+H = 128
 
 _B = {
-    "bfloat16": dict(xs=V, Pf=V + TK * R, mn=V, CS=TK * 4, m=16 * TK, ug=16 * TK, A=(16, 16), L=256, R2=512, junk=2048, I=128,
-                     Wm=16, Wc=256, Wu=(16, 16), Wy=(8, 16), Wn=(8, 16), HL=512, Ws=128, VV=16, Rep=128, WB=256, C4=4 * TK),
-    "float16": dict(XR=TK * R, XS=TK * 4, Y=TK, Rb=128, P4=512, Z=240),
-    "int32": dict(Pl=V + TK * 4, Vi=16, D6=(16, 6), pt=16, pi=8, pj=8, pk=16, p8=8, th1=8, th2=8),
-    "uint16": dict(O=TK, ix=16, fi=16, ob=8, op=2),
-    "float32": dict(U=V + TK * R, GS=TK * R, SC=256, C6=(16, 6), t1=16, t2=16, po=16, r=16, yy=16, yc=16, D1=256, Ag=256,
-                    B=256, Gt=256, F1=32, F2=32, FR=32, pf=8, PD=128, G8=256, G16=256, mk=256, Wt=(16, 16), Wv=(16, 16),
-                    mk3=(16, 16), CC=24, CD=16, Sh=128, THV=16, base=16 * R, rs=128, D0=256),
+    "bfloat16": dict(xs=V, Pf=V + TK * R, Pi=V + TK * (R + 1), mn=V, CS=TK * 4, IS=TK * R, LN=(R + 1, 16 * R),
+                     m=16 * TK, ug=16 * TK, A=(16, 16), L=512, Rr=256, junk=2048, I=128, Wm=32, Wc=256, Wu=16, Wy=(8, 16),
+                     Wn=(8, 16), HL=512, Ws=(8, 16), Wq=(8, 16), VV=16, Rep=128, WB=(16, 16), C4=8 * H, TH=256, wr=16, Wo=8,
+                     one=256, G16=256, xg=512),
+    "float16": dict(XR=TK * R, XS=TK * 4, Y=TK, Rb=256, P4=512, Z=240),
+    "int32": dict(Pl=V + TK * 4, Q=128, pi=8, pj=8, th1=8),
+    "uint16": dict(O=TK, On=H, lx=(2, 16), ob=8, oq=8),
+    "float32": dict(U=V + TK * R, SC=512, CQ=128, W=128, own=(3, 16), n2=16, n3=16, X=32, po=32, r=16, YY=48, Ag=256, B=256, Gt=128,
+                    pf=8, PD=128, G8=16, mk=16, CC=24, CD=4, base=2 * R, rs=128, i4=8, i8=8, Ft=256, Fl=128),
 }
 SCRATCH = {k: ("sbuf", [128] + (list(s) if isinstance(s, tuple) else [s]), d) for d, bufs in _B.items() for k, s in bufs.items()}
 SCRATCH.update({"ps%d" % b: ("psum", [128, 512], "float32") for b in range(8)})
-SEMAPHORES = (["sv", "sa", "st", "sg", "sent", "lva", "lvx", "lth", "lha", "o1", "o2", "o3", "arF", "rep"]
-              + ["l%s%d" % (s, i) for s in "fh" for i in range(4)] + ["ar%s%d" % (s, i) for s in "XcD" for i in range(1, R)])
+SEMAPHORES = (["sv", "sa", "st", "sg", "sent", "lva", "lvx", "lth", "lha", "lid", "o1", "o2", "o3", "rep0", "rep1"]
+              + ["l%s%d" % (s, i) for s in "fh" for i in range(4)]
+              + ["ar%s%d" % (s, i) for s in ("Xa", "Xb", "ca", "cb") for i in range(1, R)]
+              + ["ar%s%d" % (s, i) for s in "DN" for i in range(1, R + 1)] + ["arF"])
 
 ALU = AluOpType
 ACT = ActivationFunctionType
 ADD, SUB, MUL, MAX, MIN, EQ = ALU.add, ALU.subtract, ALU.mult, ALU.max, ALU.min, ALU.is_equal
 SHR, AND = ALU.arith_shift_right, ALU.bitwise_and
-RU, RPH, RPL, RFH, RFL, RONE, RID, RLEN = range(8)
-(cK1, cK2, cA, cIS, cCC, cB0, cE1, cHID, cML, cBL, cSR, cBR, cKEEP, cD1, cM10, cM15) = range(16)
+RPH, RFH, RIH, RPL, RFL, RIL, RID, RU, RONE = range(9)
+(cK1, cK2, cA, cCC, cB0, cKEEP, cSR, cBR, cML, cBL) = (0, 1, 2, 3, 4, 9, 10, 11, 12, 13)
 BANKS = ["b%d" % b for b in range(8)]
-PV = [(k, k + 1) for k in range(7)] + [(7, 11), (11, 14), (14, 15), (15, 16)]
-PA = [(0, 4), (4, 7), (7, 11), (11, 14), (14, 15), (15, 16)]
+NS = 2
+EARLY, TURN, SC = True, 0, 2
+PV = ([(0, 4), (4, 8), (8, 12), (12, 16)], [(NS, 4), (4, 8), (8, 12), (12, 14), (14, 16)])
+PV0 = ([(0, 1), (1, 4), (4, 8), (8, 12), (12, 16)], PV[1])
+VT = [(0, 0, 1), (0, 2, 4), (0, 6, 8), (1, 6, 8)]
+PA = [(0, 8), (8, 14), (14, 16)]
 
 
 def rank_program(g, core, T, topo):
@@ -84,7 +92,7 @@ def rank_program(g, core, T, topo):
         note((sem, final[sem], "dma", dict(seen[e])), r, w)
 
     def send(dst, sem, out, in_, r):
-        deps("g", [r], ())
+        deps("g", r.split(), ())
         rid, pid = topo.addr(dst, core)
         g.remote_dma(out, in_, T.sem[sem], T.sem.sent, pid, rid, topo.mask(core, dst))
         sent[0] += len(topo.engines(core, dst))
@@ -130,282 +138,436 @@ def rank_program(g, core, T, topo):
         o, b, cm = {"eq": (ALU.not_equal, -row, 1), "lt": (ALU.is_ge, -row, 1), "ge": (ALU.is_gt, row, -1)}[cmp]
         op("g", lambda: g.affine_select(ap, ap, [[step, c1 + 1 - c0]], o, float(val), b, cm), ks, ks)
 
+    def weight(ap, row, val, w):
+        op("g", lambda: g.affine_select(ap, ap, [[16, 8]], ALU.not_equal, float(val), row, -1), w, w)
+
+    def fill(ap, width, val, w):
+        act(ap, T.PD[:, 0:width], "PD", w, scale=0.0, bias=float(val))
+
     for i in range(R):
         e_in = len(topo.engines(T.cores[(rank - HOPS[i]) % n], core))
-        for k in (["X%d" % (i + 1), "c%d" % (i + 1), "D%d" % (i + 1)] if i + 1 < R else ["F"]):
-            lastw[k] = ("ar" + k, e_in, "far", {})
+        for k in (["Xa", "Xb", "ca", "cb", "D", "N"] if i + 1 < R else ["D", "N"]):
+            lastw[k + str(i + 1)] = ("ar" + k + str(i + 1), e_in, "far", {})
+    lastw["F"] = ("arF", e_in, "far", {})
 
-    CH = [(0, 512), (512, 1024), (1024, 1536), (1536, V)]
-    dma("s", "lva", [(T.Pl[:, V:V + TK], T.va[:])], "", "l0")
+    CH = [(0, 384), (384, 896), (896, 1408), (1408, V)]
     for i, (lo, hi) in enumerate(CH):
         dma("a", "lh%d" % i, [(T.Pf[:, lo:hi], T.hx[:, lo:hi])], "", "h%d" % i)
         dma("s", "lf%d" % i, [(T.xs[:, lo:hi], T.fx[:, lo:hi])], "", "f%d" % i)
-    dma("s", "lvx", [(T.Pf[:, V:V + TK], T.vx[:])], "", "c0")
-    dma("s", "lth", [(T.th1[0:1, 0:8], T.th[:])], "", "th1")
+        if i == 0:
+            dma("s", "lth", [(T.th1[0:1, 0:8], T.th[:])], "", "th1")
+        if i == 1:
+            dma("s", "lva", [(T.Pl[:, V:V + TK], T.va[:])], "", "la0 lb0")
+            dma("s", "lvx", [(T.Pf[:, V:V + TK], T.vx[:])], "", "ca0 cb0")
     FX, HX = names("f", 0, 4), names("h", 0, 4)
 
     ms(T.VV[0:16, :], 0.0, names("V", 0, 16))
     ms(T.HL[0:64, :], 0.0, "HL")
     iint(T.pi[:, 0:1], [[0, 1]], 0, 1, "pi")
     iota(T.PD[:, :], [[1, 128]], 0, -1, "PD")
-    iota(T.G8[:, :], [[0, 32], [1, 8]], 0, 0, "G8")
+    iota(T.G8[:, :], [[0, 2], [1, 8]], 0, 0, "G8")
     iota(T.Gt[0:16, 0:128], [[0, 8], [1, 16]], 0, -1, "Gt")
+    sel(cA, cA, RIH + 1, 1, cmp="lt")
+    sel(cCC, cB0 + R - 1, RONE, 1, cmp="ge")
     sel(cK1, cK2, RU, 65536)
-    sel(cA, cA, RPH, 1)
-    sel(cIS, cB0, RONE, 1)
-    sel(cK1, cK2, RFH, 128, step=RFH - RPH)
-    sel(cA, cA, RFH, 1)
-    sel(cCC, cB0, RLEN, 1024)
-    sel(cK1, cK2, RFL, 1, step=RFL - RPL)
     sel(cA, cA, RID, 128)
     sel(cCC, cCC, RID, V * rank)
+    sel(cK1, cK2, RFH, 128, step=RFH - RPH)
+    sel(cCC, cCC, RPH, -MID / 128)
+    sel(cK1, cK2, RFL, 1, step=RFL - RPL)
+    sel(cCC, cCC, RFL, 1)
+    sel(cK1, cK2, RONE, -65536)
+    sel(cCC, cCC, RIH, V // 128 * rank)
+    sel(cK1, cK2, RONE + 1, -8 * 4096)
     iota(T.G16[:, :], [[0, 2], [1, 8], [0, 16]], 0, 0, "G16")
-    iota(T.Wt[:], [[-4096, 16], [0, 16]], 61440, 0, "Wt")
-    iota(T.mk3[:], [[0, 32], [1, 8]], 0, 0, "mk3")
     for j in range(4):
         act(T.HL[0:1, 128 * j:128 * j + 128], T.PD[0:1, :], "PD HL", "HA+")
         if j:
             act(T.HL[32:33, 128 * j:128 * j + 128], T.PD[32:33, :], "PD HL", "HA+", scale=0.0, bias=float(j))
 
-    ms(T.Ws[0:64, :], 0.0, "Ws")
+    ms(T.Ws[0:64], 0.0, "Ws")
     ms(T.Wy[:], 0.0, "Wy")
     ms(T.Wn[:], 0.0, "Wn")
-    for row in (RPL, RFL, RID):
-        ms(T.Ws[0:1, row::16], 1.0, "Ws" if row == RPL else "Ws+")
-    for row, val in ((RPH, 1.0), (RFH, 1.0), (RID, 128.0)):
-        ms(T.Ws[32:33, row::16], val, "Ws+")
+    ms(T.Ws[0:1, :, RPL:RID + 1], 1.0, "Ws")
+    ms(T.Ws[32:33, :, RPH:RIH + 1], 1.0, "Ws+")
+    ms(T.Ws[32:33, :, RID], 128.0, "Ws+")
     ts(T.pj[:, 0:1], T.pi[:, 0:1], 4, SHR, "pi", "pj0")
     ts(T.pj[:, 1:2], T.pi[:, 0:1], 4, SHR, "pi", "pj1", 1, AND)
     ts(T.I[:, :], T.PD[:, :], 0.0, EQ, "PD", "I")
     cp(T.pf[:, 0:2], T.pj[:, 0:2], "pj0 pj1", "pf")
+    ts(T.Rep[0:16, 0:128], T.Gt[0:16, 0:128], 0.0, EQ, "Gt", "Rep")
+    ts(T.mk[:, 0:16], T.G8[:, 0:16], T.pf[:, 0:1], EQ, "G8 pf", "mk")
+    ms(T.TH[0:1, :], 0.0, "TH")
+    cp(T.Wy[:, :, RU], T.mk[:, 0:8], "mk", "Wy")
+    ts(T.Wn[:, :, RU], T.mk[:, 0:8], -2.0, MUL, "mk", "Wn")
+    ms(T.wr[0:1, 0:16], 0.0, "wr")
+    ms(T.Wq[0:1], 0.0, "Wq")
+    ms(T.one[0:1, :], 1.0, "one")
+    ms(T.wr[0:1, cK1:cK2 + 1], -65536.0, "wr")
+    ms(T.Wq[0:1, :, RIH], float((n * V + rank * TK) // 128), "Wq")
     ts(T.pf[:, 2:3], T.pf[:, 1:2], 0.0, EQ, "pf", "pe")
+    ms(T.wr[0:1, cB0:cB0 + R], -1.0, "wr")
     par = [T.pf[:, 2:3], T.pf[:, 1:2]]
     for e in (1, 0):
         for gp in range(2):
             j = 2 * e + gp
             ts(T.P4[:, 128 * j:128 * j + 128], T.PD[:, :], float(16 * (gp - e)), EQ, "PD pf" if e else "PD pe", "P4+", par[e], MUL)
-    ts(T.mk[:, :], T.G8[:, :], T.pf[:, 0:1], EQ, "G8 pf", "mk")
-    ts(T.Rep[0:16, :], T.Gt[0:16, 0:128], 0.0, EQ, "Gt", "Rep")
-    cp(T.Wy[:, :, RU], T.mk[:, 0:8], "mk", "Wy")
-    ts(T.Wn[:, :, RU], T.mk[:, 0:8], -2.0, MUL, "mk", "Wn")
-    cp(T.XR[:, 0:TK], T.Pl[:, V:V + TK], "l0", "X0")
-    mm(ps[3][:, 0:5], T.Rep[0:16, :], T.VV[0:16, 0:5], True, True, "Rep" + names("V", 0, 5), "b3")
-    act(T.CC[:, 0:5], ps[3][:, 0:5], "", "CC0 b3")
-    for i in range(4):
-        act(T.CD[:, i:i + 1], col(cA), "CC0", "CD%d" % i, scale=float(4 * i), bias=col(cCC))
+    cp(T.TH[0:1, RONE:128:16], T.th1[0:1, 0:8], "th1 TH", "TH1")
+    cp(T.TH[0:1, 128 + RU:256:16], T.th1[0:1, 0:8], "th1 TH", "TH2")
+    ts(T.pj[:, 2:3], T.pi[:, 0:1], 8, AND, "pi", "q2")
+    ts(T.pj[:, 3:4], T.pi[:, 0:1], 7, AND, "pi", "q3")
+    ts(T.i8[:, :], T.G8[:, 0:8], 32.0, MUL, "G8", "i8", 15.0, ADD)
+    cp(T.pf[:, 3:5], T.pj[:, 2:4], "q2 q3", "pq")
+    ts(T.oq[:, :], T.i8[:, :], T.pf[:, 3:4], ADD, "i8 pq", "oq", T.pf[:, 3:4], ADD)
+    ts(T.pf[:, 5:6], T.pf[:, 4:5], T.pf[:, 0:1], EQ, "pq pf", "pq5")
+    ts(T.i4[:, :], T.G8[:, 0:8], T.pf[:, 3:4], ADD, "G8 pq", "i4", -16.0, ADD)
 
-    def turn_lists(i):
-        for h in range(2):
-            tr(T.Y[:, h::2], T.XR[:, TK * i + 128 * h:TK * i + 128 * h + 128], "X%d" % i, "Y%d" % h)
-        for b in range(4):
+    def offset_constants():
+        ts(T.ob[:, :], T.i4[:, :], T.pf[:, 5:6], MUL, "i4 pq5", "ob", 16.0, ADD)
+        ts(T.Z[:, :], T.G16[:, 0:240], 0.0, MUL, "G16", "Z")
+
+    for i, (lo, hi) in enumerate(CH):
+        mm(ps[4 + i][:, 0:hi - lo], T.Ws[0:64], T.HL[0:64, 0:hi - lo], True, False, "Ws HL HA", "b%d" % (4 + i))
+    mm(ps[3][:, 0:TK], T.Ws[0:64], T.HL[0:64, 0:TK], True, False, "Ws HL HA", "b3")
+    mm(ps[3][:, 0:TK], T.Wq[0:1], T.one[0:1, :], False, True, "Wq one", "b3")
+    for j, c in enumerate((2.0 ** -16, 0.0, 2.0 ** -16, 1.0, 2.0 ** -3, 2.0 ** -6, 2.0 ** -9, 2.0 ** -12)):
+        fill(T.CQ[:, j::8], 16, c, "CQ+")
+    act(T.Pi[:, V:V + TK], ps[3][:, 0:TK], "", "D0 b3")
+
+    def turn_a(i, h):
+        for j in range(2):
+            c = TK * i + H * h + 64 * j
+            tr(T.Y[:, H * h + j:H * h + H:2], T.XR[:, c:c + 64], "X%s%d" % ("ab"[h], i), "Y%d%d" % (h, j))
+        for b in range(2):
             for e in range(2):
                 for gp in range(2):
-                    j = 2 * e + gp
-                    mm(ps[2][:, 2 * b + e:256:8], T.P4[:, 128 * j:128 * j + 128],
-                       T.Y[:, 64 * b + 32 * gp:64 * b + 32 * gp + 32], gp == 0, gp == 1, "P4 Y0 Y1", "b2")
-        if 0 < i < R - 1:
-            cp(T.Pl[:, V + TK * i:V + TK * (i + 1)], T.XR[:, TK * i:TK * (i + 1)], "X%d" % i, "l%d" % i)
-        cp(T.O[:, :], ps[2][:, 0:256], "", "O b2")
+                    j, c = 2 * e + gp, H * h + 64 * b + 32 * gp
+                    mm(ps[2 + h][:, 2 * b + e:H:4], T.P4[:, 128 * j:128 * j + 128], T.Y[:, c:c + 32], gp == 0, gp == 1,
+                       "P4 Y%d0 Y%d1" % (h, h), "b%d" % (2 + h))
 
-    turn_lists(0)
+    def turn_b(h):
+        cp(T.O[:, H * h:H * h + H], ps[2 + h][:, 0:H], "", "O%d b%d" % (h, 2 + h))
 
     def homes(i):
-        mm(ps[i % 2][:, 0:CH[i][1] - CH[i][0]], T.I[:, :], T.Pf[:, CH[i][0]:CH[i][1]], True, True, "I h%d" % i, "b%d" % (i % 2))
+        lo, hi = CH[i]
+        mm(ps[i % 2][:, 0:hi - lo], T.I[:, :], T.Pf[:, lo:hi], True, True, "I h%d" % i, "b%d" % (i % 2))
+        mm(ps[4 + i][:, 0:hi - lo], T.Wy[:], T.Pf[:, lo:hi], False, False, "Wy h%d" % i, "b%d" % (4 + i))
 
-    homes(0)
-    homes(1)
-    for i, (lo, hi) in enumerate(CH):
+    def table(i):
+        lo, hi = CH[i]
         tt(T.mn[:, lo:hi], T.xs[:, lo:hi], ps[i % 2][:, 0:hi - lo], MIN, "f%d" % i, "mn%d b%d" % (i, i % 2))
         o, bk = ps[4 + i][:, 0:hi - lo], "b%d" % (4 + i)
-        mm(o, T.Ws[0:64, :], T.HL[0:64, 0:hi - lo], True, False, "Ws HL HA", bk)
-        mm(o, T.Wy[:], T.Pf[:, lo:hi], False, False, "Wy h%d" % i, bk)
+        mm(o, T.Wn[:], T.mn[:, lo:hi], False, True, "Wn mn%d" % i, bk)
         if i < 2:
             homes(i + 2)
-        mm(o, T.Wn[:], T.mn[:, lo:hi], False, True, "Wn mn%d" % i, bk)
         act(T.U[:, lo:hi], o, "CD%d" % i, "U+ " + bk, bias=T.CD[:, i:i + 1])
-    ts(T.Wm[:, :], T.mk[:, 0:16], 131072.0, MUL, "mk", "Wm")
-    ts(T.Wc[:, :], T.G16[:, :], T.pf[:, 0:1], EQ, "G16 pf", "Wc", -65536.0, MUL)
-    ts(T.mk3[:], T.mk3[:], T.pf[:, 0:1], EQ, "mk3 pf", "mk3")
-    for K in range(2):
-        ts(T.Wv[:, :, 8 * K:8 * K + 8], T.Wt[:, :, 8 * K:8 * K + 8], col(cIS), MUL, "Wt CC0", "Wv+", col(cK1 + K), ADD)
 
-    sel(cB0, cB0, RPH, 13)
-    sel(cE1, cE1, RPH, 1)
-    sel(cHID, cHID, RID, 1)
-    sel(cML, cML, 6, 1, cmp="ge")
-    sel(cBL, cBL, 6, 1, cmp="lt")
-    sel(cSR, cSR, 10, 2.0 ** 29, cmp="lt")
-    sel(cBR, cBR, 10, -2.0 ** 20, cmp="ge")
+    homes(0)
+    mm(ps[2][:, 0:4], T.Rep[0:16, 0:128], T.VV[0:16, 0:4], True, False, "Rep" + names("V", 0, 4), "b2")
+    mm(ps[2][:, 0:4], T.TH[0:1, 0:128], T.wr[0:1, 0:4], False, True, "TH1 wr", "b2")
+    homes(1)
+    act(T.CC[:, 0:4], ps[2][:, 0:4], "", "CC0 b2")
+    for i in range(4):
+        act(T.CD[:, i:i + 1], col(cA), "CC0", "CD%d" % i, scale=float(CH[i][0] // 128), bias=col(cCC))
+    table(0)
+    ts(T.Wm[:, 0:16], T.mk[:, 0:16], 131072.0, MUL, "mk", "Wm+")
+    ts(T.Wm[:, 16:32], T.mk[:, 0:16], -131072.0, MUL, "mk", "Wm+")
+    ts(T.Wc[:, :], T.G16[:, :], T.pf[:, 0:1], EQ, "G16 pf", "Wc", -65536.0, MUL)
+    table(1)
+    cp(T.XR[:, 0:TK], T.Pl[:, V:V + TK], "la0", "Xa0 Xb0")
+    turn_a(0, 0)
+    offset_constants()
+    table(2)
+    turn_b(0)
+    turn_a(0, 1)
+    table(3)
+    for K in range(2):
+        ts(T.Wu[:, 8 * K:8 * K + 8], T.mk[:, 0:8], col(cK1 + K), MUL, "mk CC0", "Wu+")
+    turn_b(1)
+
+    iota(T.rs[:, :], [[0, 128]], 4096, 0, "rs")
+    op("g", lambda: g.affine_select(T.rs[:, 0::16], T.rs[:, 0::16], [[0, 8]], ALU.is_gt, -2.0 ** 26, 0, 0), "rs", "rs")
+    iota(T.W[:, 127:128], [[0, 1]], 0, 0, "W0")
+    iota(T.A[:, :, 15], [[-128, 2], [0, 8]], 255, -1, "Att")
+    sel(cML, cML, 11, 1, cmp="lt")
+    sel(cSR, cSR, 11, -2.0 ** 28, cmp="ge")
+    sel(cBR, cBR, 11, -2.0 ** 28, cmp="lt")
     sel(cKEEP, cKEEP, RU, 1)
-    sel(cD1, cD1, 0, 2.0 ** 20, cmp="ge")
-    sel(cM10, cM15, 10, -1, step=-5)
-    sel(cB0, cB0, RPL, 255)
-    sel(cSR, cSR, 6, 2.0 ** 20, cmp="lt")
-    sel(cBR, cBR, 11, -2.0 ** 28, cmp="ge")
+    sel(cB0, cB0 + R - 1, RPL, 255)
+    sel(cML, cML, 1, 0)
+    sel(cBL, cBL, 11, 1, cmp="ge")
+    sel(cSR, cSR, 7, 2.0 ** 29, cmp="lt")
+    sel(cBR, cBR, 7, 0, cmp="lt")
     sel(cKEEP, cKEEP, RFH, 1)
-    sel(cD1, cD1, RLEN, 1)
-    sel(cSR, cSR, 5, 2.0 ** 12, cmp="lt")
-    sel(cBR, cBR, 15, -2.0 ** 12, cmp="ge")
+    sel(cB0, cB0 + R - 1, RU, -1)
+    sel(cSR, cSR, 3, 0, cmp="lt")
+    sel(cBR, cBR, 0, -2.0 ** 20)
     sel(cKEEP, cKEEP, RFL, 1)
-    sel(cSR, cSR, 4, -2.0 ** 28, cmp="lt")
-    iota(T.base[:, :], [[TK, R], [128, 2], [0, 8]], V - MID, 1, "base")
-    iota(T.D0[:, :], [[1, TK]], n * V + rank * TK, 0, "D00")
-    for j in (4, 15):
-        iota(T.A[:, :, j], [[-128, 2], [0, 8]], 255, -1, "Att+")
-    iint(T.pk[:, :], [[-1, 16]], 16, 1, "pk")
-    iint(T.p8[:, :], [[1, 8]], 0, 0, "p8")
-    op("g", lambda: g.partition_broadcast(T.th2[:, :], T.th1[0:1, :], 128), "th1 p8", "th2")
+    sel(cBL, cBL, 1, 1)
+    sel(cSR, cSR, 1, -2.0 ** 17)
+    sel(cML, cML, 2, 0)
+    for i in range(R):
+        sel(cB0 + i, cB0 + i, RPH, (V + TK * i - MID) / 128)
+    sel(cSR, cSR, 15, 2.0 ** 12)
+    iota(T.own[:, 0:2, :], [[MID + 1, 2], [0, 16]], -MID - 1, 0, "own")
+    dma("g", "lid", [(T.Pi[:, 0:V], T.U[:, 0:V])], "U", "Pi")
+    for h in range(2):
+        iota(T.own[:, 2, h:h + 1], [[0, 1]], -4096 * (255 - H * h), 4096, "ow2+")
+    for j, (h, lo, hi) in enumerate(VT):
+        iota(T.own[:, 0:2, 8 * h + lo:8 * h + hi], [[MID + 1, 2], [0, hi - lo]], -MID - 1 - 4096 * (255 - H * h), 4096, "own+" if j else "own")
+    iota(T.YY[:, :], [[0, 48]], 0, 0, "y00 y01 y10 y11")
+    iota(T.base[:, 0:2 * R], [[TK, R], [H, 2]], V - MID, 1, "base")
+    iota(T.WB[:], [[0, 256]], 0, 0, "WB0 WB1")
+    iota(T.Wo[:, :], [[0, 8]], 0, 0, "Wo")
+    weight(T.WB[:, 0:8, RU], 1, -2.0 ** -20, "WB0")
+    weight(T.WB[:, 8:16, RIH], RIH, 1, "WB1")
+    weight(T.WB[:, 0:8, RPL], 15, -2.0 ** -12, "WB0")
+    weight(T.WB[:, 8:16, RIL], RIL, 1, "WB1")
+    weight(T.Wo[:, :], RIH, 128, "Wo")
+    weight(T.WB[:, 8:16, RID], RIH, 128, "WB1")
+    weight(T.Wo[:, :], RIL, 1, "Wo")
+    weight(T.WB[:, 8:16, RID], RIL, 1, "WB1")
+    iota(T.U[:, V:V + TK], [[0, TK]], 0, 0, "Ud")
 
     def late_constants():
-        mm(ps[3][:, 8:19], T.Rep[0:16, :], T.VV[0:16, 5:16], True, True, "Rep" + names("V", 5, 16), "b3")
-        act(T.CC[:, 5:16], ps[3][:, 8:19], "", "CC1 b3")
+        mm(ps[2][:, 0:10], T.Rep[0:16, 0:128], T.VV[0:16, 4:14], True, False, "Rep" + names("V", 4, 14), "b2")
+        mm(ps[2][:, 0:10], T.TH[0:1, 128:256], T.wr[0:1, 4:14], False, True, "TH2 wr", "b2")
+        mm(ps[3][:, 0:16], T.Rep[0:16, 0:128], T.Rep[0:16, 0:16], True, True, "Rep", "b3")
+        cp(T.CC[:, 4:14], ps[2][:, 0:10], "", "CC1 b2")
+        cp(T.Z[:, 112:128], ps[3][:, 0:16], "", "Z b3")
         for e in range(2):
-            act(T.CC[:, 16 + 2 * e:18 + 2 * e], T.CC[:, cSR:cBR + 1], "CC1 pf pe", "CR+", scale=par[e])
-        act(T.U[:, V:V + TK], T.D0[:, :], "D00 CC1", "D0", scale=col(cHID))
-        for i in range(R):
-            act(T.CD[:, 4 + i:5 + i], col(cE1), "CC1", "CB+", scale=float(2 * i), bias=col(cB0))
-        ms(T.rs[:, :], 0.0, "rs")
-        ms(T.C6[:], 3.5, "C6")
-        ts(T.Z[:, :], T.G8[:, 0:240], 0.0, MUL, "G8", "Z")
-        ts(T.pk[:, :], T.pk[:, :], 15, AND, "pk", "pk")
-        ms(T.rs[:, 0::16], -2.0 ** 26, "rs")
-        ms(T.C6[:, :, 0::5], 0.0, "C6")
-        for h in range(2):
-            ts(T.THV[:, 8 * h:8 * h + 8], T.th2[:, :], 1.0, ADD, "th2", "THV+", 65536.0, MUL)
-        ts(T.pj[:, 3:4], T.pi[:, 0:1], 8, AND, "pi", "q3")
-        ts(T.pj[:, 4:5], T.pi[:, 0:1], 14, AND, "pi", "q4")
-        ts(T.pj[:, 5:6], T.pi[:, 0:1], 1, AND, "pi", "q5")
-        ts(T.Z[:, 112:128], T.pk[:, :], 0.0, EQ, "pk", "Z")
-        cp(T.pf[:, 3:6], T.pj[:, 3:6], "q3 q4 q5", "pq")
-        ts(T.p8[:, :], T.p8[:, :], T.pf[:, 3:4], ADD, "p8 pq th2", "p8")
-        ts(T.pf[:, 6:7], T.pf[:, 4:5], 16.0, MUL, "pq", "pq6", T.pf[:, 5:6], ADD)
-        cp(T.ob[:, :], T.p8[:, :], "p8", "ob")
+            ts(T.CC[:, 16 + 2 * e:18 + 2 * e], T.CC[:, cML:cBL + 1], par[e], MUL, "CC1 pf pe", "CR+")
 
-    def last_constants():
-        ts(T.WB[:, 0:128], T.PD[:, :], float(RU - 10), EQ, "PD CC1", "WB+", col(cM10), MUL)
-        ts(T.WB[:, 128:256], T.PD[:, :], float(RPL - 15), EQ, "PD CC1", "WB+", col(cM15), MUL)
-        ts(T.Sh[:, :], T.PD[:, :], 0.0, EQ, "PD CC1", "Sh", col(cHID), MUL)
-        for gp in range(2):
-            ts(T.op[:, gp:gp + 1], T.pf[:, 6:7], float(RID + 16 * gp), ADD, "pq6", "op+")
+    def scan(K, h):
+        c = TK * K + H * h
+        op("v", lambda: v.tensor_tensor_scan(T.SC[:, c:c + H], T.rs[:, :], ps[h][:, H * K:H * K + H], 0.0, ADD, MAX),
+           "rs", "SC%d%d b%d" % (K, h, h))
 
-    def scans(K):
-        for h in range(2):
-            op("v", lambda: v.tensor_tensor_scan(T.SC[:, 128 * h:128 * h + 128], T.rs[:, :], ps[h][:, 128 * K:128 * K + 128],
-                                                 0.0, ADD, MAX), "rs", "SC%d b%d" % (h, h))
+    def load(b, h, towns):
+        for j, gg in enumerate(towns):
+            q, gp = gg // 2, gg % 2
+            mm(ps[b][:, TK * j:TK * j + TK], T.L[32 * q:32 * q + 32, TK * gp + H * h:TK * gp + H * h + H], T.Rr[32 * q:32 * q + 32, :],
+               True, True, "L%d%d R0 R1" % (h, gp), "b%d" % b)
 
-    def payload():
-        tt(T.t1[:, :], T.THV[:, :], T.SC[:, 15::16], SUB, "THV SC0 SC1", "t1")
-        ts(T.pt[:, :], T.Vi[:, :], 4095, AND, "Vi", "pt")
-        ts(T.t2[:, :], T.t1[:, :], 0.0, MAX, "t1", "t2", float(-MID), ADD)
-        tt(T.po[:, :], T.t2[:, :], T.pt[:, :], ADD, "t2 pt", "po")
+    def reduce(b, h, towns):
+        for j, gg in enumerate(towns):
+            s = 8 * h + gg
+            src = ps[b][:, TK * j:TK * j + TK]
+            if b < 6:
+                op("v", lambda: v.tensor_reduce(T.r[:, s:s + 1], src, AxisListType.X, MAX), "", "rv%d+ b%d" % (h, b))
+            else:
+                act(T.junk[:, TK * gg:TK * gg + TK], src, "ow2", "ra%d+ jk%d b%d" % (h, gg, b), func=ACT.Relu, accum_out=T.r[:, s:s + 1],
+                    bias=T.own[:, 2, h:h + 1])
 
-    def offsets(i, out, key, b, meanwhile=None):
-        tt(T.yy[:, :], T.r[:, :], T.po[:, :], ADD, "rv ra po", "yy")
-        tt(T.yc[:, :], T.yy[:, :], T.base[:, 16 * i:16 * i + 16], MIN, "yy base", "yc")
-        tt(T.Rb[:, :], T.yc[:, :].indirect(T.ob[:, :]), T.mk[:, 0:128], MUL, "yc ob mk", "Rb")
+    def list_a(i, h):
+        for K in range(2):
+            tt(T.YY[:, 24 * h + 8 * K:24 * h + 8 * K + 8], T.r[:, 8 * h:8 * h + 8], T.po[:, 16 * K + 8 * h:16 * K + 8 * h + 8], ADD,
+               "rv%d ra%d po" % (h, h), "y%d%d" % (h, K))
+        ts(T.Rb[:, H * h:H * h + H], T.YY[:, 24 * h:24 * h + 24].indirect(T.ob[:, :]), T.base[:, 2 * i + h:2 * i + h + 1], MIN,
+           "y%d0 y%d1 ob base" % (h, h), "Rb%d" % h)
         for gg in range(8):
-            mm(ps[b][:, 0:16], T.Z[:, 112 - 16 * gg:240 - 16 * gg], T.Rb[:, 16 * gg:16 * gg + 16], gg == 0, gg == 7, "Z Rb", "b%d" % b)
-        if meanwhile:
-            meanwhile()
-        ts(out[:, :], ps[b][:, 0:16], float(MID), ADD, "", "%s b%d" % (key, b))
+            mm(ps[h][:, 0:16], T.Z[:, 112 - 16 * gg:240 - 16 * gg], T.Rb[:, H * h + 16 * gg:H * h + 16 * gg + 16], gg == 0, gg == 7,
+               "Z Rb%d" % h, "b%d" % h)
 
+    def list_b(h):
+        ts(T.lx[:, :, 8 * h:8 * h + 8], ps[h][:, 0:16], float(MID), ADD, "", "ix%d b%d" % (h, h))
+
+    def pool(i):
+        c = TK * i
+        if i < R - 1:
+            op("g", lambda: g.affine_select(T.Pl[:, V + c:V + c + TK], T.XR[:, c:c + TK], [[0, TK]], ALU.is_ge, 0.0, 0, 0),
+               "Xa%d Xb%d" % (i, i), "la%d lb%d" % (i, i))
+        iota(T.U[:, V + c:V + c + TK], [[0, TK]], 0, 0, "Ud")
+
+    def u_sum(h, k, src, key):
+        mm(ps[h][:, k:TK:16], src, T.Wu[:, :], False, k == 15, key + " Wu", "b%d" % h)
+
+    later = []
     for i in range(R):
         last = i == R - 1
         dst = T.cores[(rank + HOPS[i]) % n]
         c0 = V + TK * i
-        mine = slice(TK * i, TK * (i + 1))
-        dma("s", "rep", [(T.C4[:, TK * j:TK * (j + 1)], T.Pf[:, c0:c0 + TK]) for j in range(4)], "c%d" % i, "C4")
+        def copies(h):
+            for j in range(2):
+                act(T.C4[:, H * (4 * h + j):H * (4 * h + j + 1)], T.Pf[:, c0 + H * h:c0 + H * h + H], "c%s%d" % ("ab"[h], i), "C4%d+" % h)
+            act(T.C4[:, H * (4 * h + 2):H * (4 * h + 4)], T.C4[:, H * 4 * h:H * (4 * h + 2)], "C4%d" % h, "C4%d+" % h)
+
+        for h in range(SC * int(i > 0), 2):
+            dma("s", "rep%d" % h, [(T.C4[:, H * (4 * h + j):H * (4 * h + j + 1)], T.Pf[:, c0 + H * h:c0 + H * h + H]) for j in range(4)],
+                "c%s%d" % ("ab"[h], i), "C4%d" % h)
+        if i and SC:
+            copies(0)
         if i == 0:
             dma("s", "lha", [(T.Pl[:, 0:V], T.ha[:])], "f3 h3", "Pl")
+        if i:
+            act(T.ug[:, 0:16 * H], T.U[:, 0:V].indirect(T.On[:, :]), "U On", names("ug0", 0, 16), func=ACT.Copy)
         else:
-            turn_lists(i)
+            act(T.ug[:, 0:16 * H], T.U[:, 0:V].indirect(T.O[:, 0:H]), "U O0", names("ug0", 0, 16), func=ACT.Copy)
         for h in range(2):
-            mm(ps[h][:, 0:256], T.Pf[:, c0 + 128 * h:c0 + 128 * h + 128], T.Wc[:, :], True, False, "c%d Wc" % i, "b%d" % h)
-        for k1, key, k0 in sorted([(k1, "m", k0) for k0, k1 in PV] + [(k1, "ug", k0) for k0, k1 in PA]):
-            off = T.O[:, 16 * k0:16 * k1]
-            if key == "ug":
-                act(T.ug[:, TK * k0:TK * k1], T.U[:, 0:V].indirect(off), "U O", names("ug", k0, k1), func=ACT.Copy)
-            elif k1 - k0 == 1:
-                tt(T.m[:, TK * k0:TK * k1], T.xs[:, :].indirect(off), T.Pf[:, c0:c0 + TK], MIN, FX + "O c%d" % i, "m%d" % k0)
-            else:
-                tt(T.m[:, TK * k0:TK * k1], T.xs[:, :].indirect(off), T.C4[:, 0:TK * (k1 - k0)], MIN, FX + "O C4", names("m", k0, k1))
-            if i == 0 and k1 == 1:
-                tt(T.Wu[:], T.Wv[:], T.mk3[:], MUL, "Wv mk3", "Wu")
-            for k in range(k0, k1):
-                for h in range(2):
-                    mm(ps[h][:, k:256:16], T[key][:, TK * k + 128 * h:TK * k + 128 * h + 128],
-                       T.Wm[:, :] if key == "m" else T.Wu[:, k, :], False, k == 15 and key == "ug",
-                       "%s%d W%s" % (key, k, key[0]), "b%d" % h)
-        if i == 0:
-            late_constants()
-        act(T.D1[:, :], T.U[:, c0:c0 + TK], "D%d CC1" % i, "Dp", bias=col(cD1))
-        scans(0 if last else 1)
-        cp(T.Vi[:, :], T.SC[:, 15::16], "SC0 SC1", "Vi")
-        for j, sh in enumerate((9, 6, 3)):
-            ts(T.D6[:, :, 1 + j], T.Vi[:, :], sh, SHR, "Vi", "d%d" % (1 + j), 7, AND)
-        ts(T.D6[:, :, 4], T.Vi[:, :], 7, AND, "Vi", "d4")
-        for j in (0, 5):
-            ts(T.D6[:, :, j], T.Vi[:, :], 16, SHR, "Vi", "d%d" % j)
-        tt(T.A[:, :, 5:11], T.D6[:], T.C6[:], SUB, names("d", 0, 6) + "C6", "Ad")
-        for j in (0, 11):
-            tt(T.A[:, :, j:j + 4], T.A[:, :, 6:10], T.A[:, :, 6:10], MUL, "Ad", "As%d" % j)
-        for b in (3, 2):
-            for h in range(2):
-                mm(ps[b][:, 128 * h:128 * h + 128], T.A[:, 8 * h:8 * h + 8, :], T.I[:, :], True, True, "Ad As0 As11 Att I", "b%d" % b)
-        payload()
-        ts(T.R2[:, 0:256], ps[3][:, 0:256], col(16), MUL, "CR", "R0 b3", col(17), ADD)
-        act(T.L[:, 0:128], ps[2][:, 0:128], "CC1", "L0 b2", scale=col(cML), bias=col(cBL))
-        act(T.R2[:, 256:512], ps[2][:, 0:256], "CR", "R1 b2", scale=col(18), bias=col(19))
-        ts(T.L[:, 128:256], ps[3][:, 128:256], col(cML), MUL, "CC1", "L1 b3", col(cBL), ADD)
-        for h in range(2):
-            for q in range(4):
-                bk = "b%d" % (4 + q)
-                mm(ps[4 + q][:, :], T.L[32 * q:32 * q + 32, 128 * h:128 * h + 128], T.R2[32 * q:32 * q + 32, :], True, True,
-                   "L%d R0 R1" % h, bk)
-                for gp in range(2):
-                    s = 8 * h + 2 * q + gp
-                    src = ps[4 + q][:, 256 * gp:256 * gp + 256]
-                    if q % 2 == 1:
-                        op("v", lambda: v.tensor_reduce(T.r[:, s:s + 1], src, AxisListType.X, MAX), "", "rv+ " + bk)
-                    else:
-                        j = TK * (s // 4 * 2 + gp)
-                        act(T.junk[:, j:j + TK], src, "", "ra+ " + bk, func=ACT.Relu, accum_out=T.r[:, s:s + 1])
+            cs = "c%s%d" % ("ab"[h], i)
+            if h == 0:
+                mm(ps[0][:, 0:TK], T.Pf[:, c0:c0 + H], T.Wc[:, :], True, False, cs + " Wc", "b0")
+            todo = list(PA)
+            w = H * NS
+
+            def second_half():
+                cb = "cb%d" % i
+                if i and SC == 2:
+                    copies(1)
+                act(T.xg[:, 0:w], T.xs[:, :].indirect(T.O[:, H:H + 8 * NS]), FX + "O1", "xg", scale=-1.0)
+                mm(ps[1][:, 0:TK], T.Pf[:, c0 + H:c0 + TK], T.Wc[:, :], True, False, cb + " Wc", "b1")
+                for k in range(NS):
+                    mm(ps[1][:, k:TK:16], T.Pf[:, c0 + H:c0 + TK], T.Wm[:, 0:16], False, False, cb + " Wm", "b1")
+                    mm(ps[4][:, H * k:H * k + H], T.I[:, :], T.Pf[:, c0 + H:c0 + TK], k == 0, False, "I " + cb, "b4")
+                mm(ps[4][:, 0:w], T.I[:, :], T.xg[:, 0:w], False, True, "I xg", "b4")
+
+            for j, (k0, k1) in enumerate((PV if i else PV0)[h]):
+                m0 = H * (16 * h + k0)
+                wide = k1 - k0 > 1
+                tt(T.m[:, m0:m0 + H * (k1 - k0)], T.xs[:, :].indirect(T.O[:, H * h + 8 * k0:H * h + 8 * k1]),
+                   T.C4[:, 4 * H * h:4 * H * h + H * (k1 - k0)] if wide else T.Pf[:, c0 + H * h:c0 + H * h + H], MIN,
+                   FX + "O%d " % h + ("C4%d" % h if wide else cs), names("m%d" % h, k0, k1))
+                if i and (h, j) == (0, TURN):
+                    turn_a(i, 1)
+                if i and (h, j) == (0, TURN + 1):
+                    turn_b(1)
+                    pool(i)
+                    while later:
+                        send(*later.pop(0))
+                for k in range(k0, k1):
+                    mm(ps[h][:, k:TK:16], T.m[:, H * (16 * h + k):H * (16 * h + k + 1)], T.Wm[:, 0:16], False, False, "m%d%d Wm" % (h, k), "b%d" % h)
+                if (h, k1) == (0, 12):
+                    second_half()
+                if (h, j) == (1, 1):
+                    scan(0, 0)
+                    scan(1, 0)
+                if i == 0 and (h, j) == (1, 2):
+                    late_constants()
+                while h and todo and todo[0][1] <= k1:
+                    u0, u1 = todo.pop(0)
+                    act(T.ug[:, H * (16 + u0):H * (16 + u1)], T.U[:, 0:V].indirect(T.O[:, H + 8 * u0:H + 8 * u1]), "U O1",
+                        names("ug1", u0, u1), func=ACT.Copy)
+                    if u0 == 0:
+                        act(T.m[:, 16 * H:16 * H + w], ps[4][:, 0:w], "", names("m1", 0, NS) + "b4", func=ACT.Relu)
+                        for k in range(NS):
+                            mm(ps[1][:, k:TK:16], T.m[:, H * (16 + k):H * (17 + k)], T.Wm[:, 16:32], False, False, "m1%d Wm" % k, "b1")
+                    for k in range(u0, u1):
+                        u_sum(1, k, T.ug[:, H * (16 + k):H * (17 + k)], "ug1%d" % k)
+            if h == 0:
+                for k in range(16):
+                    u_sum(0, k, T.ug[:, k:16 * H:16] if i else T.ug[:, H * k:H * k + H], "ug0%d" % k)
+        scan(0, 1)
+        tt(T.Q[:, :], T.SC[:, 0:TK].indirect(T.oq[:, :]), T.CQ[:, :], MUL, "SC00 SC01 oq CQ", "Q")
+        ts(T.W[:, 0:127], T.Q[:, 1:128], 8.0, MUL, "Q", "W")
+        tt(T.A[:, :, 0:8], T.Q[:, :], T.W[:, :], SUB, "Q W W0", "Ad As0")
+        tt(T.A[:, :, 7:11], T.A[:, :, 3:7], T.A[:, :, 3:7], MUL, "Ad", "As0")
+        act(T.A[:, :, 11:15], T.A[:, :, 3:7], "Ad", "As1", func=ACT.Square)
+        for b, h in ((2, 0), (3, 1), (3, 0)):
+            mm(ps[b][:, H * h:H * h + H], T.A[:, 8 * h:8 * h + 8, :], T.I[:, :], True, True, "Ad As0 As1 Att I", "b%d" % b)
+        ts(T.n2[:, :], T.Q[:, 0::8], -8192.0, MUL, "Q", "n2", 0.0, MAX)
+        ts(T.n3[:, :], T.Q[:, 7::8], -4096.0, MUL, "Q", "n3")
+        scan(1, 1)
+        tt(T.n2[:, :], T.n2[:, :], T.n3[:, :], ADD, "n2 n3", "n2")
+        ts(T.Rr[:, 0:H], ps[2][:, 0:H], col(cSR), MUL, "CC1", "R0 b2", col(cBR), ADD)
+        act(T.Rr[:, H:TK], ps[3][:, H:TK], "CC1", "R1 b3", scale=col(cSR), bias=col(cBR))
+        ts(T.L[:, 0:H], ps[2][:, 0:H], col(16), MUL, "CR", "L00 b2", col(17), ADD)
+        act(T.L[:, TK:TK + H], ps[3][:, 0:H], "CR", "L01 b3", scale=col(18), bias=col(19))
+        for gp in range(2):
+            act(T.L[:, TK * gp + H:TK * gp + TK], ps[3][:, H:TK], "CR", "L1%d b3" % gp, scale=col(16 + 2 * gp), bias=col(17 + 2 * gp))
+        for K in range(2):
+            tt(T.X[:, 16 * K:16 * K + 16], T.n2[:, :], T.own[:, K, :], ADD, "n2 own", "X+")
+        load(4, 0, (0,))
+        load(5, 0, (2, 3))
+        load(6, 0, (1,))
+        load(7, 0, (4, 5))
+        tt(T.po[:, :], T.SC[:, 15::16], T.X[:, :], ADD, "SC00 SC01 SC10 SC11 X", "po")
+        reduce(4, 0, (0,))
+        load(4, 0, (6, 7))
+        reduce(6, 0, (1,))
+        load(6, 1, (0, 1))
+        reduce(5, 0, (2, 3))
+        reduce(7, 0, (4, 5))
+        load(7, 1, (2, 3))
+        reduce(4, 0, (6, 7))
+        reduce(6, 1, (0, 1))
+        pools = HX + names("ca", 0, i + 1) + names("cb", 0, i + 1)
+        lists = " Pl" + names("la", 0, i + 1) + names("lb", 0, i + 1)
+        ids = "Pi" + names("D", 0, i + 1)
+        e0 = TK * i
+
+        def leave(h):
+            a0 = TK * i + H * h
+            cp(T.XS[:, a0:a0 + H], T.Pl[:, 0:c0 + TK].indirect(T.lx[:, 1, 8 * h:8 * h + 8]), "ix%d" % h + lists, "XS%d%d" % (i, h))
+            send(dst, "arX%s%d" % ("ab"[h], i + 1), T.XR[:, a0 + TK:a0 + TK + H], T.XS[:, a0:a0 + H], "XS%d%d" % (i, h))
+
+        def feats(h):
+            a0 = TK * i + H * h
+            act(T.CS[:, a0:a0 + H], T.Pf[:, 0:c0 + TK].indirect(T.lx[:, 1, 8 * h:8 * h + 8]), "ix%d" % h + pools, "CS%d%d" % (i, h), func=ACT.Copy)
+            send(dst, "arc%s%d" % ("ab"[h], i + 1), T.Pf[:, c0 + TK + H * h:c0 + TK + H * h + H], T.CS[:, a0:a0 + H], "CS%d%d" % (i, h))
+
+        load(5, 1, (6,))
+        list_a(i, 0)
+        reduce(5, 1, (6,))
+        load(6, 1, (4, 5))
+        load(4, 1, (7,))
+        mm(ps[3][:, 0:TK], T.WB[:, 0:8, :], T.Rr[:, :], True, False, "WB0 R0 R1", "b3")
+        mm(ps[3][:, 0:TK], T.WB[:, 8:16, :], T.Pi[:, c0:c0 + TK], False, True, "WB1 D%d" % i, "b3")
+        list_b(0)
         if not last:
-            offsets(i, T.ix, "ix", 2, lambda: scans(0))
-            cp(T.XS[:, mine], T.Pl[:, 0:c0 + TK].indirect(T.ix[:, :]), "ix Pl" + names("l", 0, i + 1), "XS%d" % i)
-            act(T.CS[:, mine], T.Pf[:, 0:c0 + TK].indirect(T.ix[:, :]), "ix" + HX + names("c", 0, i + 1), "CS%d" % i, func=ACT.Copy)
-            send(dst, "arX%d" % (i + 1), T.XR[:, TK * (i + 1):TK * (i + 2)], T.XS[:, mine], "XS%d" % i)
-            send(dst, "arc%d" % (i + 1), T.Pf[:, c0 + TK:c0 + 2 * TK], T.CS[:, mine], "CS%d" % i)
-            cp(T.Vi[:, :], T.SC[:, 15::16], "SC0 SC1", "Vi")
-            payload()
+            leave(0)
+        else:
+            cp(T.IS[:, e0:e0 + H], T.Pi[:, 0:c0 + TK].indirect(T.lx[:, 1, 0:8]), "ix0 " + ids, "IS%d" % i)
+            send(dst, "arF", T.Pi[:, c0 + TK:c0 + TK + H], T.IS[:, e0:e0 + H], "IS%d" % i)
+        reduce(7, 1, (2, 3))
+        if EARLY and not last:
+            feats(0)
+        reduce(4, 1, (7,))
+        reduce(6, 1, (4, 5))
+        list_a(i, 1)
+        win, fi = T.U[:, 0:c0 + TK], T.lx[:, 0, :]
 
         def new_rows():
-            if i == 0:
-                last_constants()
-            mm(ps[6][:, 0:256], T.WB[:, 0:128], T.L[:, :], True, False, "WB L0 L1", "b6")
-            mm(ps[6][:, 0:256], T.WB[:, 128:256], T.L[:, :], False, False, "WB L0 L1", "b6")
-            mm(ps[6][:, 0:256], T.Sh[:, :], T.U[:, c0:c0 + TK], False, True, "Sh D%d" % i, "b6")
-            act(T.B[:, :], ps[6][:, 0:256], "CB", "B b6", bias=T.CD[:, 4 + i:5 + i])
+            act(T.B[:, :], ps[3][:, 0:TK], "CC1", "B b3", bias=col(cB0 + i))
+
+        def lengths():
+            for h in range(2):
+                act(T.LN[:, i, 16 * i + h:16 * i + 16:2], T.YY[:, 24 * h:24 * h + 8], "y%d0 base" % h, "tk%d%d" % (i, h), func=ACT.Sign,
+                    scale=-1.0, bias=T.base[:, 2 * i + h:2 * i + h + 1])
+            args = (dst, "arN%d" % (i + 1), T.LN[:, i + 1, 0:16 * i + 16], T.LN[:, i, 0:16 * i + 16], "tk%d0 tk%d1 N%d" % (i, i, i))
+            send(*args) if last else later.append(args)
 
         if not last:
+            if not EARLY:
+                feats(0)
             new_rows()
-        offsets(i, T.fi, "fi", 3, new_rows if last else None)
-        olds = names("D", 0, i + 1)
-        win = T.U[:, 0:c0 + TK]
-        act(T.Ag[:, :], win.indirect(T.fi[:, :]), "U fi CC1" + olds, "Ag", scale=col(cKEEP))
-        tt(T.GS[:, mine], win.indirect(T.fi[:, :]), T.D1[:, :], MIN, "U fi Dp" + olds, "G%d" % i)
-        if not last:
-            send(dst, "arD%d" % (i + 1), T.U[:, c0 + TK:c0 + 2 * TK], T.GS[:, mine], "G%d" % i)
+            lengths()
+            list_b(1)
+            act(T.Ag[:, :], win.indirect(fi), "U Ud ix0 ix1 CC1", "Ag", scale=col(cKEEP))
+            leave(1)
+            feats(1)
+            tt(win.indirect(fi), T.Ag[:, :], T.B[:, :], ADD, "Ag B ix0 ix1", "U Ud")
+            act(T.IS[:, e0:e0 + TK], T.Pi[:, 0:c0 + TK].indirect(T.lx[:, 1, :]), "ix0 ix1 " + ids, "IS%d" % i, func=ACT.Copy)
+            later.append((dst, "arD%d" % (i + 1), T.Pi[:, c0 + TK:c0 + 2 * TK], T.IS[:, e0:e0 + TK], "IS%d C41" % i))
+            turn_a(i + 1, 0)
+            cp(T.On[:, :], T.XR[:, e0 + TK:e0 + TK + H], "Xa%d" % (i + 1), "On")
+            turn_b(0)
         else:
-            tr(T.Gt[:, :], T.GS[:, mine], "G%d" % i, "Gt")
-            cp(T.F1[:, :], T.Gt[:, :].indirect(T.op[:, :]), "Gt op", "F1")
-            tr(T.F2[:, :], T.F1[:, :], "F1", "F2")
-            send(dst, "arF", T.FR[:, :], T.F2[:, :], "F2")
-        tt(win.indirect(T.fi[:, :]), T.Ag[:, :], T.B[:, :], ADD, "Ag B fi", "U" + olds)
+            lengths()
+            new_rows()
+            list_b(1)
+            act(T.IS[:, e0 + H:e0 + TK], T.Pi[:, 0:c0 + TK].indirect(T.lx[:, 1, 8:16]), "ix1 " + ids, "IT", func=ACT.Copy)
+            send(dst, "arD%d" % R, T.Pi[:, c0 + TK + H:c0 + 2 * TK], T.IS[:, e0 + H:e0 + TK], "IT")
+            cp(win.indirect(fi), T.B[:, :], "B ix0 ix1", "U Ud")
 
     dma("s", "o1", [(T.yh[:], T.U[RID::16, 0:V])], "U", "")
-    dma("a", "o2", [(T.yt[:], T.FR[0::2, :])], "F", "")
-    dma("s", "o3", [(T.yl[:], T.FR[1::2, :])], "F", "")
+    c0 = V + TK * R
+    for i in range(R):
+        mm(ps[5][0:16, 0:H], T.LN[:, R, 16 * i:16 * i + 16], T.I[:, :], i == 0, i == R - 1, "I N%d" % R, "b5")
+    mm(ps[4][0:8, 0:TK], T.Wo[:, :], T.Pi[:, c0:c0 + TK], True, True, "Wo F D%d" % R, "b4")
+    act(T.Ft[0:8, :], ps[4][0:8, 0:TK], "", "Ft b4")
+    ts(T.Fl[0:16, :], ps[5][0:16, 0:H], 0.5, MUL, "", "Fl b5", R / 2, ADD)
+    dma("a", "o2", [(T.yt[:], T.Ft[0:8, :])], "Ft", "")
+    dma("s", "o3", [(T.yl[:], T.Fl[0:16, :])], "Fl", "")
     for e in cnt:
         wait("g", ("s" + e, cnt[e], e, {}))
     wait("g", ("sent", sent[0], "g", {}))

from concourse.mybir import AluOpType, ActivationFunctionType, AxisListType

V, TK, HOPS = 1664, 256, (1, 2, 3, 2, 1)
R = len(HOPS)
MID = 1472
H = 128

_B = {
    "bfloat16": dict(xs=V, Pf=V + TK * R, Pi=V + TK * (R + 1), mn=V, CS=TK * 4, IS=TK * R, LN=(R + 1, 16 * R),
                     m=16 * TK, ug=16 * TK, A=(16, 16), L=512, Rr=256, junk=2048, I=128, Wm=32, Wc=256, Wu=16, Wy=(8, 16),
                     Wn=(8, 16), HL=512, Ws=(8, 16), Wq=(8, 16), VV=16, Rep=128, WB=(16, 16), C4=8 * H, TH=256, wr=16, Wo=8,
                     one=256, G16=256, xg=512),
    "float16": dict(XR=TK * R, XS=TK * 4, Y=TK, Rb=256, P4=512, Z=240),
    "int32": dict(Pl=V + TK * 4, Q=128, pi=8, pj=8, th1=8),
    "uint16": dict(O=TK, On=H, lx=(2, 16), ob=8, oq=8),
    "float32": dict(U=V + TK * R, SC=512, CQ=128, W=128, own=(3, 16), n2=16, n3=16, X=32, po=32, r=16, YY=48, Ag=256, B=256, Gt=128,
                    pf=8, PD=128, G8=16, mk=16, CC=24, CD=4, base=2 * R, rs=128, i4=8, i8=8, Ft=256, Fl=128),
}
SCRATCH = {k: ("sbuf", [128] + (list(s) if isinstance(s, tuple) else [s]), d) for d, bufs in _B.items() for k, s in bufs.items()}
SCRATCH.update({"ps%d" % b: ("psum", [128, 512], "float32") for b in range(8)})
SEMAPHORES = (["sv", "sa", "st", "sg", "sent", "lva", "lvx", "lth", "lha", "lid", "o1", "o2", "o3", "rep0", "rep1"]
              + ["l%s%d" % (s, i) for s in "fh" for i in range(4)]
              + ["ar%s%d" % (s, i) for s in ("Xa", "Xb", "ca", "cb") for i in range(1, R)]
              + ["ar%s%d" % (s, i) for s in "DN" for i in range(1, R + 1)] + ["arF"])

ALU = AluOpType
ACT = ActivationFunctionType
ADD, SUB, MUL, MAX, MIN, EQ = ALU.add, ALU.subtract, ALU.mult, ALU.max, ALU.min, ALU.is_equal
SHR, AND = ALU.arith_shift_right, ALU.bitwise_and
RPH, RFH, RIH, RPL, RFL, RIL, RID, RU, RONE = range(9)
(cK1, cK2, cA, cCC, cB0, cKEEP, cSR, cBR, cML, cBL) = (0, 1, 2, 3, 4, 9, 10, 11, 12, 13)
BANKS = ["b%d" % b for b in range(8)]
NS = 2
EARLY, TURN, SC = True, 0, 2
PV = ([(0, 4), (4, 8), (8, 12), (12, 16)], [(NS, 4), (4, 8), (8, 12), (12, 14), (14, 16)])
PV0 = ([(0, 1), (1, 4), (4, 8), (8, 12), (12, 16)], PV[1])
VT = [(0, 0, 1), (0, 2, 4), (0, 6, 8), (1, 6, 8)]
PA = [(0, 8), (8, 14), (14, 16)]


def rank_program(g, core, T, topo):
    rank = T.rank_of(core)
    if rank is None:
        return
    n = len(T.cores)
    v, a, t = g.vector, g.scalar, g.tensor
    Q = {"v": v, "a": a, "t": t, "g": g, "s": g.sync}
    cnt = {"v": 0, "a": 0, "t": 0, "g": 0}
    seen = {e: {} for e in Q}
    lastw, readers, final, sent = {}, {}, {}, [0]
    ps = [T["ps%d" % b] for b in range(8)]

    def wait(e, tok):
        if seen[e].get(tok[0], 0) < tok[1]:
            Q[e].wait_ge(T.sem[tok[0]], tok[1])
            seen[e][tok[0]] = tok[1]
            for s, c in tok[3].items():
                seen[e][s] = max(seen[e].get(s, 0), c)

    def deps(e, r, w):
        toks = [lastw[k] for k in r if k in lastw]
        for k in w:
            part = k.endswith("+")
            k = k.rstrip("+")
            own = part or k in BANKS
            if k in lastw and not (own and lastw[k][2] == e):
                toks.append(lastw[k])
            toks += readers.get(k, [])
        for tok in sorted(toks, key=lambda x: -x[1]):
            wait(e, tok)

    def note(tok, r, w):
        for k in r:
            readers.setdefault(k, []).append(tok)
        for k in w:
            lastw[k.rstrip("+")] = tok
            readers[k.rstrip("+")] = []

    def op(e, fn, r, w):
        r, w = r.split(), w.split()
        deps(e, r, w)
        cnt[e] += 1
        fn().then_inc(T.sem["s" + e], 1)
        note(("s" + e, cnt[e], e, dict(seen[e])), r, w)

    def dma(e, sem, pairs, r, w):
        r, w = r.split(), w.split()
        deps(e, r, w)
        for out, in_ in pairs:
            Q[e].dma_start(out, in_).then_inc(T.sem[sem], 16)
            final[sem] = final.get(sem, 0) + 16
        note((sem, final[sem], "dma", dict(seen[e])), r, w)

    def send(dst, sem, out, in_, r):
        deps("g", r.split(), ())
        rid, pid = topo.addr(dst, core)
        g.remote_dma(out, in_, T.sem[sem], T.sem.sent, pid, rid, topo.mask(core, dst))
        sent[0] += len(topo.engines(core, dst))

    def ts(out, in0, s1, o0, r, w, s2=None, o1=None):
        if o1 is None:
            op("v", lambda: v.tensor_scalar(out, in0, s1, None, o0), r, w)
        else:
            op("v", lambda: v.tensor_scalar(out, in0, s1, s2, o0, o1), r, w)

    def tt(out, in0, in1, o, r, w):
        op("v", lambda: v.tensor_tensor(out, in0, in1, o), r, w)

    def cp(out, in_, r, w):
        op("v", lambda: v.tensor_copy(out, in_), r, w)

    def tr(out, in_, r, w):
        op("v", lambda: v.transpose(out, in_), r, w)

    def ms(ap, c, w):
        op("v", lambda: v.memset(ap, c), "", w)

    def act(out, in_, r, w, func=ACT.Identity, **kw):
        op("a", lambda: a.activation(out, in_, func, **kw), r, w)

    def mm(out, lhsT, rhs, start, stop, r, x):
        op("t", lambda: t.matmul(out, lhsT, rhs, start, stop), r, x)

    def iota(out, pat, base, cm, w):
        op("g", lambda: g.iota(out, pat, base, cm, allow_small_or_imprecise_dtypes=True), "", w)

    def iint(out, pat, base, cm, w):
        op("g", lambda: g.iota(out, pat, base, cm), "", w)

    def col(c):
        return T.CC[:, c:c + 1]

    def names(p, lo, hi):
        return " " + " ".join("%s%d" % (p, j) for j in range(lo, hi)) + " "

    def sel(c0, c1, row, val, step=0, cmp="eq"):
        ap, ks = T.VV[0:16, c0:c1 + 1], names("V", c0, c1 + 1)
        o, b, cm = {"eq": (ALU.not_equal, -row, 1), "lt": (ALU.is_ge, -row, 1), "ge": (ALU.is_gt, row, -1)}[cmp]
        op("g", lambda: g.affine_select(ap, ap, [[step, c1 + 1 - c0]], o, float(val), b, cm), ks, ks)

    def weight(ap, row, val, w):
        op("g", lambda: g.affine_select(ap, ap, [[16, 8]], ALU.not_equal, float(val), row, -1), w, w)

    def fill(ap, width, val, w):
        act(ap, T.PD[:, 0:width], "PD", w, scale=0.0, bias=float(val))

    for i in range(R):
        e_in = len(topo.engines(T.cores[(rank - HOPS[i]) % n], core))
        for k in (["Xa", "Xb", "ca", "cb", "D", "N"] if i + 1 < R else ["D", "N"]):
            lastw[k + str(i + 1)] = ("ar" + k + str(i + 1), e_in, "far", {})
    lastw["F"] = ("arF", e_in, "far", {})

    CH = [(0, 384), (384, 896), (896, 1408), (1408, V)]
    for i, (lo, hi) in enumerate(CH):
        dma("a", "lh%d" % i, [(T.Pf[:, lo:hi], T.hx[:, lo:hi])], "", "h%d" % i)
        dma("s", "lf%d" % i, [(T.xs[:, lo:hi], T.fx[:, lo:hi])], "", "f%d" % i)
        if i == 0:
            dma("s", "lth", [(T.th1[0:1, 0:8], T.th[:])], "", "th1")
        if i == 1:
            dma("s", "lva", [(T.Pl[:, V:V + TK], T.va[:])], "", "la0 lb0")
            dma("s", "lvx", [(T.Pf[:, V:V + TK], T.vx[:])], "", "ca0 cb0")
    FX, HX = names("f", 0, 4), names("h", 0, 4)

    ms(T.VV[0:16, :], 0.0, names("V", 0, 16))
    ms(T.HL[0:64, :], 0.0, "HL")
    iint(T.pi[:, 0:1], [[0, 1]], 0, 1, "pi")
    iota(T.PD[:, :], [[1, 128]], 0, -1, "PD")
    iota(T.G8[:, :], [[0, 2], [1, 8]], 0, 0, "G8")
    iota(T.Gt[0:16, 0:128], [[0, 8], [1, 16]], 0, -1, "Gt")
    sel(cA, cA, RIH + 1, 1, cmp="lt")
    sel(cCC, cB0 + R - 1, RONE, 1, cmp="ge")
    sel(cK1, cK2, RU, 65536)
    sel(cA, cA, RID, 128)
    sel(cCC, cCC, RID, V * rank)
    sel(cK1, cK2, RFH, 128, step=RFH - RPH)
    sel(cCC, cCC, RPH, -MID / 128)
    sel(cK1, cK2, RFL, 1, step=RFL - RPL)
    sel(cCC, cCC, RFL, 1)
    sel(cK1, cK2, RONE, -65536)
    sel(cCC, cCC, RIH, V // 128 * rank)
    sel(cK1, cK2, RONE + 1, -8 * 4096)
    iota(T.G16[:, :], [[0, 2], [1, 8], [0, 16]], 0, 0, "G16")
    for j in range(4):
        act(T.HL[0:1, 128 * j:128 * j + 128], T.PD[0:1, :], "PD HL", "HA+")
        if j:
            act(T.HL[32:33, 128 * j:128 * j + 128], T.PD[32:33, :], "PD HL", "HA+", scale=0.0, bias=float(j))

    ms(T.Ws[0:64], 0.0, "Ws")
    ms(T.Wy[:], 0.0, "Wy")
    ms(T.Wn[:], 0.0, "Wn")
    ms(T.Ws[0:1, :, RPL:RID + 1], 1.0, "Ws")
    ms(T.Ws[32:33, :, RPH:RIH + 1], 1.0, "Ws+")
    ms(T.Ws[32:33, :, RID], 128.0, "Ws+")
    ts(T.pj[:, 0:1], T.pi[:, 0:1], 4, SHR, "pi", "pj0")
    ts(T.pj[:, 1:2], T.pi[:, 0:1], 4, SHR, "pi", "pj1", 1, AND)
    ts(T.I[:, :], T.PD[:, :], 0.0, EQ, "PD", "I")
    cp(T.pf[:, 0:2], T.pj[:, 0:2], "pj0 pj1", "pf")
    ts(T.Rep[0:16, 0:128], T.Gt[0:16, 0:128], 0.0, EQ, "Gt", "Rep")
    ts(T.mk[:, 0:16], T.G8[:, 0:16], T.pf[:, 0:1], EQ, "G8 pf", "mk")
    ms(T.TH[0:1, :], 0.0, "TH")
    cp(T.Wy[:, :, RU], T.mk[:, 0:8], "mk", "Wy")
    ts(T.Wn[:, :, RU], T.mk[:, 0:8], -2.0, MUL, "mk", "Wn")
    ms(T.wr[0:1, 0:16], 0.0, "wr")
    ms(T.Wq[0:1], 0.0, "Wq")
    ms(T.one[0:1, :], 1.0, "one")
    ms(T.wr[0:1, cK1:cK2 + 1], -65536.0, "wr")
    ms(T.Wq[0:1, :, RIH], float((n * V + rank * TK) // 128), "Wq")
    ts(T.pf[:, 2:3], T.pf[:, 1:2], 0.0, EQ, "pf", "pe")
    ms(T.wr[0:1, cB0:cB0 + R], -1.0, "wr")
    par = [T.pf[:, 2:3], T.pf[:, 1:2]]
    for e in (1, 0):
        for gp in range(2):
            j = 2 * e + gp
            ts(T.P4[:, 128 * j:128 * j + 128], T.PD[:, :], float(16 * (gp - e)), EQ, "PD pf" if e else "PD pe", "P4+", par[e], MUL)
    cp(T.TH[0:1, RONE:128:16], T.th1[0:1, 0:8], "th1 TH", "TH1")
    cp(T.TH[0:1, 128 + RU:256:16], T.th1[0:1, 0:8], "th1 TH", "TH2")
    ts(T.pj[:, 2:3], T.pi[:, 0:1], 8, AND, "pi", "q2")
    ts(T.pj[:, 3:4], T.pi[:, 0:1], 7, AND, "pi", "q3")
    ts(T.i8[:, :], T.G8[:, 0:8], 32.0, MUL, "G8", "i8", 15.0, ADD)
    cp(T.pf[:, 3:5], T.pj[:, 2:4], "q2 q3", "pq")
    ts(T.oq[:, :], T.i8[:, :], T.pf[:, 3:4], ADD, "i8 pq", "oq", T.pf[:, 3:4], ADD)
    ts(T.pf[:, 5:6], T.pf[:, 4:5], T.pf[:, 0:1], EQ, "pq pf", "pq5")
    ts(T.i4[:, :], T.G8[:, 0:8], T.pf[:, 3:4], ADD, "G8 pq", "i4", -16.0, ADD)

    def offset_constants():
        ts(T.ob[:, :], T.i4[:, :], T.pf[:, 5:6], MUL, "i4 pq5", "ob", 16.0, ADD)
        ts(T.Z[:, :], T.G16[:, 0:240], 0.0, MUL, "G16", "Z")

    for i, (lo, hi) in enumerate(CH):
        mm(ps[4 + i][:, 0:hi - lo], T.Ws[0:64], T.HL[0:64, 0:hi - lo], True, False, "Ws HL HA", "b%d" % (4 + i))
    mm(ps[3][:, 0:TK], T.Ws[0:64], T.HL[0:64, 0:TK], True, False, "Ws HL HA", "b3")
    mm(ps[3][:, 0:TK], T.Wq[0:1], T.one[0:1, :], False, True, "Wq one", "b3")
    for j, c in enumerate((2.0 ** -16, 0.0, 2.0 ** -16, 1.0, 2.0 ** -3, 2.0 ** -6, 2.0 ** -9, 2.0 ** -12)):
        fill(T.CQ[:, j::8], 16, c, "CQ+")
    act(T.Pi[:, V:V + TK], ps[3][:, 0:TK], "", "D0 b3")

    def turn_a(i, h):
        for j in range(2):
            c = TK * i + H * h + 64 * j
            tr(T.Y[:, H * h + j:H * h + H:2], T.XR[:, c:c + 64], "X%s%d" % ("ab"[h], i), "Y%d%d" % (h, j))
        for b in range(2):
            for e in range(2):
                for gp in range(2):
                    j, c = 2 * e + gp, H * h + 64 * b + 32 * gp
                    mm(ps[2 + h][:, 2 * b + e:H:4], T.P4[:, 128 * j:128 * j + 128], T.Y[:, c:c + 32], gp == 0, gp == 1,
                       "P4 Y%d0 Y%d1" % (h, h), "b%d" % (2 + h))

    def turn_b(h):
        cp(T.O[:, H * h:H * h + H], ps[2 + h][:, 0:H], "", "O%d b%d" % (h, 2 + h))

    def homes(i):
        lo, hi = CH[i]
        mm(ps[i % 2][:, 0:hi - lo], T.I[:, :], T.Pf[:, lo:hi], True, True, "I h%d" % i, "b%d" % (i % 2))
        mm(ps[4 + i][:, 0:hi - lo], T.Wy[:], T.Pf[:, lo:hi], False, False, "Wy h%d" % i, "b%d" % (4 + i))

    def table(i):
        lo, hi = CH[i]
        tt(T.mn[:, lo:hi], T.xs[:, lo:hi], ps[i % 2][:, 0:hi - lo], MIN, "f%d" % i, "mn%d b%d" % (i, i % 2))
        o, bk = ps[4 + i][:, 0:hi - lo], "b%d" % (4 + i)
        mm(o, T.Wn[:], T.mn[:, lo:hi], False, True, "Wn mn%d" % i, bk)
        if i < 2:
            homes(i + 2)
        act(T.U[:, lo:hi], o, "CD%d" % i, "U+ " + bk, bias=T.CD[:, i:i + 1])

    homes(0)
    mm(ps[2][:, 0:4], T.Rep[0:16, 0:128], T.VV[0:16, 0:4], True, False, "Rep" + names("V", 0, 4), "b2")
    mm(ps[2][:, 0:4], T.TH[0:1, 0:128], T.wr[0:1, 0:4], False, True, "TH1 wr", "b2")
    homes(1)
    act(T.CC[:, 0:4], ps[2][:, 0:4], "", "CC0 b2")
    for i in range(4):
        act(T.CD[:, i:i + 1], col(cA), "CC0", "CD%d" % i, scale=float(CH[i][0] // 128), bias=col(cCC))
    table(0)
    ts(T.Wm[:, 0:16], T.mk[:, 0:16], 131072.0, MUL, "mk", "Wm+")
    ts(T.Wm[:, 16:32], T.mk[:, 0:16], -131072.0, MUL, "mk", "Wm+")
    ts(T.Wc[:, :], T.G16[:, :], T.pf[:, 0:1], EQ, "G16 pf", "Wc", -65536.0, MUL)
    table(1)
    cp(T.XR[:, 0:TK], T.Pl[:, V:V + TK], "la0", "Xa0 Xb0")
    turn_a(0, 0)
    offset_constants()
    table(2)
    turn_b(0)
    turn_a(0, 1)
    table(3)
    for K in range(2):
        ts(T.Wu[:, 8 * K:8 * K + 8], T.mk[:, 0:8], col(cK1 + K), MUL, "mk CC0", "Wu+")
    turn_b(1)

    iota(T.rs[:, :], [[0, 128]], 4096, 0, "rs")
    op("g", lambda: g.affine_select(T.rs[:, 0::16], T.rs[:, 0::16], [[0, 8]], ALU.is_gt, -2.0 ** 26, 0, 0), "rs", "rs")
    iota(T.W[:, 127:128], [[0, 1]], 0, 0, "W0")
    iota(T.A[:, :, 15], [[-128, 2], [0, 8]], 255, -1, "Att")
    sel(cML, cML, 11, 1, cmp="lt")
    sel(cSR, cSR, 11, -2.0 ** 28, cmp="ge")
    sel(cBR, cBR, 11, -2.0 ** 28, cmp="lt")
    sel(cKEEP, cKEEP, RU, 1)
    sel(cB0, cB0 + R - 1, RPL, 255)
    sel(cML, cML, 1, 0)
    sel(cBL, cBL, 11, 1, cmp="ge")
    sel(cSR, cSR, 7, 2.0 ** 29, cmp="lt")
    sel(cBR, cBR, 7, 0, cmp="lt")
    sel(cKEEP, cKEEP, RFH, 1)
    sel(cB0, cB0 + R - 1, RU, -1)
    sel(cSR, cSR, 3, 0, cmp="lt")
    sel(cBR, cBR, 0, -2.0 ** 20)
    sel(cKEEP, cKEEP, RFL, 1)
    sel(cBL, cBL, 1, 1)
    sel(cSR, cSR, 1, -2.0 ** 17)
    sel(cML, cML, 2, 0)
    for i in range(R):
        sel(cB0 + i, cB0 + i, RPH, (V + TK * i - MID) / 128)
    sel(cSR, cSR, 15, 2.0 ** 12)
    iota(T.own[:, 0:2, :], [[MID + 1, 2], [0, 16]], -MID - 1, 0, "own")
    dma("g", "lid", [(T.Pi[:, 0:V], T.U[:, 0:V])], "U", "Pi")
    for h in range(2):
        iota(T.own[:, 2, h:h + 1], [[0, 1]], -4096 * (255 - H * h), 4096, "ow2+")
    for j, (h, lo, hi) in enumerate(VT):
        iota(T.own[:, 0:2, 8 * h + lo:8 * h + hi], [[MID + 1, 2], [0, hi - lo]], -MID - 1 - 4096 * (255 - H * h), 4096, "own+" if j else "own")
    iota(T.YY[:, :], [[0, 48]], 0, 0, "y00 y01 y10 y11")
    iota(T.base[:, 0:2 * R], [[TK, R], [H, 2]], V - MID, 1, "base")
    iota(T.WB[:], [[0, 256]], 0, 0, "WB0 WB1")
    iota(T.Wo[:, :], [[0, 8]], 0, 0, "Wo")
    weight(T.WB[:, 0:8, RU], 1, -2.0 ** -20, "WB0")
    weight(T.WB[:, 8:16, RIH], RIH, 1, "WB1")
    weight(T.WB[:, 0:8, RPL], 15, -2.0 ** -12, "WB0")
    weight(T.WB[:, 8:16, RIL], RIL, 1, "WB1")
    weight(T.Wo[:, :], RIH, 128, "Wo")
    weight(T.WB[:, 8:16, RID], RIH, 128, "WB1")
    weight(T.Wo[:, :], RIL, 1, "Wo")
    weight(T.WB[:, 8:16, RID], RIL, 1, "WB1")
    iota(T.U[:, V:V + TK], [[0, TK]], 0, 0, "Ud")

    def late_constants():
        mm(ps[2][:, 0:10], T.Rep[0:16, 0:128], T.VV[0:16, 4:14], True, False, "Rep" + names("V", 4, 14), "b2")
        mm(ps[2][:, 0:10], T.TH[0:1, 128:256], T.wr[0:1, 4:14], False, True, "TH2 wr", "b2")
        mm(ps[3][:, 0:16], T.Rep[0:16, 0:128], T.Rep[0:16, 0:16], True, True, "Rep", "b3")
        cp(T.CC[:, 4:14], ps[2][:, 0:10], "", "CC1 b2")
        cp(T.Z[:, 112:128], ps[3][:, 0:16], "", "Z b3")
        for e in range(2):
            ts(T.CC[:, 16 + 2 * e:18 + 2 * e], T.CC[:, cML:cBL + 1], par[e], MUL, "CC1 pf pe", "CR+")

    def scan(K, h):
        c = TK * K + H * h
        op("v", lambda: v.tensor_tensor_scan(T.SC[:, c:c + H], T.rs[:, :], ps[h][:, H * K:H * K + H], 0.0, ADD, MAX),
           "rs", "SC%d%d b%d" % (K, h, h))

    def load(b, h, towns):
        for j, gg in enumerate(towns):
            q, gp = gg // 2, gg % 2
            mm(ps[b][:, TK * j:TK * j + TK], T.L[32 * q:32 * q + 32, TK * gp + H * h:TK * gp + H * h + H], T.Rr[32 * q:32 * q + 32, :],
               True, True, "L%d%d R0 R1" % (h, gp), "b%d" % b)

    def reduce(b, h, towns):
        for j, gg in enumerate(towns):
            s = 8 * h + gg
            src = ps[b][:, TK * j:TK * j + TK]
            if b < 6:
                op("v", lambda: v.tensor_reduce(T.r[:, s:s + 1], src, AxisListType.X, MAX), "", "rv%d+ b%d" % (h, b))
            else:
                act(T.junk[:, TK * gg:TK * gg + TK], src, "ow2", "ra%d+ jk%d b%d" % (h, gg, b), func=ACT.Relu, accum_out=T.r[:, s:s + 1],
                    bias=T.own[:, 2, h:h + 1])

    def list_a(i, h):
        for K in range(2):
            tt(T.YY[:, 24 * h + 8 * K:24 * h + 8 * K + 8], T.r[:, 8 * h:8 * h + 8], T.po[:, 16 * K + 8 * h:16 * K + 8 * h + 8], ADD,
               "rv%d ra%d po" % (h, h), "y%d%d" % (h, K))
        ts(T.Rb[:, H * h:H * h + H], T.YY[:, 24 * h:24 * h + 24].indirect(T.ob[:, :]), T.base[:, 2 * i + h:2 * i + h + 1], MIN,
           "y%d0 y%d1 ob base" % (h, h), "Rb%d" % h)
        for gg in range(8):
            mm(ps[h][:, 0:16], T.Z[:, 112 - 16 * gg:240 - 16 * gg], T.Rb[:, H * h + 16 * gg:H * h + 16 * gg + 16], gg == 0, gg == 7,
               "Z Rb%d" % h, "b%d" % h)

    def list_b(h):
        ts(T.lx[:, :, 8 * h:8 * h + 8], ps[h][:, 0:16], float(MID), ADD, "", "ix%d b%d" % (h, h))

    def pool(i):
        c = TK * i
        if i < R - 1:
            op("g", lambda: g.affine_select(T.Pl[:, V + c:V + c + TK], T.XR[:, c:c + TK], [[0, TK]], ALU.is_ge, 0.0, 0, 0),
               "Xa%d Xb%d" % (i, i), "la%d lb%d" % (i, i))
        iota(T.U[:, V + c:V + c + TK], [[0, TK]], 0, 0, "Ud")

    def u_sum(h, k, src, key):
        mm(ps[h][:, k:TK:16], src, T.Wu[:, :], False, k == 15, key + " Wu", "b%d" % h)

    later = []
    for i in range(R):
        last = i == R - 1
        dst = T.cores[(rank + HOPS[i]) % n]
        c0 = V + TK * i
        def copies(h):
            for j in range(2):
                act(T.C4[:, H * (4 * h + j):H * (4 * h + j + 1)], T.Pf[:, c0 + H * h:c0 + H * h + H], "c%s%d" % ("ab"[h], i), "C4%d+" % h)
            act(T.C4[:, H * (4 * h + 2):H * (4 * h + 4)], T.C4[:, H * 4 * h:H * (4 * h + 2)], "C4%d" % h, "C4%d+" % h)

        for h in range(SC * int(i > 0), 2):
            dma("s", "rep%d" % h, [(T.C4[:, H * (4 * h + j):H * (4 * h + j + 1)], T.Pf[:, c0 + H * h:c0 + H * h + H]) for j in range(4)],
                "c%s%d" % ("ab"[h], i), "C4%d" % h)
        if i and SC:
            copies(0)
        if i == 0:
            dma("s", "lha", [(T.Pl[:, 0:V], T.ha[:])], "f3 h3", "Pl")
        if i:
            act(T.ug[:, 0:16 * H], T.U[:, 0:V].indirect(T.On[:, :]), "U On", names("ug0", 0, 16), func=ACT.Copy)
        else:
            act(T.ug[:, 0:16 * H], T.U[:, 0:V].indirect(T.O[:, 0:H]), "U O0", names("ug0", 0, 16), func=ACT.Copy)
        for h in range(2):
            cs = "c%s%d" % ("ab"[h], i)
            if h == 0:
                mm(ps[0][:, 0:TK], T.Pf[:, c0:c0 + H], T.Wc[:, :], True, False, cs + " Wc", "b0")
            todo = list(PA)
            w = H * NS

            def second_half():
                cb = "cb%d" % i
                if i and SC == 2:
                    copies(1)
                act(T.xg[:, 0:w], T.xs[:, :].indirect(T.O[:, H:H + 8 * NS]), FX + "O1", "xg", scale=-1.0)
                mm(ps[1][:, 0:TK], T.Pf[:, c0 + H:c0 + TK], T.Wc[:, :], True, False, cb + " Wc", "b1")
                for k in range(NS):
                    mm(ps[1][:, k:TK:16], T.Pf[:, c0 + H:c0 + TK], T.Wm[:, 0:16], False, False, cb + " Wm", "b1")
                    mm(ps[4][:, H * k:H * k + H], T.I[:, :], T.Pf[:, c0 + H:c0 + TK], k == 0, False, "I " + cb, "b4")
                mm(ps[4][:, 0:w], T.I[:, :], T.xg[:, 0:w], False, True, "I xg", "b4")

            for j, (k0, k1) in enumerate((PV if i else PV0)[h]):
                m0 = H * (16 * h + k0)
                wide = k1 - k0 > 1
                tt(T.m[:, m0:m0 + H * (k1 - k0)], T.xs[:, :].indirect(T.O[:, H * h + 8 * k0:H * h + 8 * k1]),
                   T.C4[:, 4 * H * h:4 * H * h + H * (k1 - k0)] if wide else T.Pf[:, c0 + H * h:c0 + H * h + H], MIN,
                   FX + "O%d " % h + ("C4%d" % h if wide else cs), names("m%d" % h, k0, k1))
                if i and (h, j) == (0, TURN):
                    turn_a(i, 1)
                if i and (h, j) == (0, TURN + 1):
                    turn_b(1)
                    pool(i)
                    while later:
                        send(*later.pop(0))
                for k in range(k0, k1):
                    mm(ps[h][:, k:TK:16], T.m[:, H * (16 * h + k):H * (16 * h + k + 1)], T.Wm[:, 0:16], False, False, "m%d%d Wm" % (h, k), "b%d" % h)
                if (h, k1) == (0, 12):
                    second_half()
                if (h, j) == (1, 1):
                    scan(0, 0)
                    scan(1, 0)
                if i == 0 and (h, j) == (1, 2):
                    late_constants()
                while h and todo and todo[0][1] <= k1:
                    u0, u1 = todo.pop(0)
                    act(T.ug[:, H * (16 + u0):H * (16 + u1)], T.U[:, 0:V].indirect(T.O[:, H + 8 * u0:H + 8 * u1]), "U O1",
                        names("ug1", u0, u1), func=ACT.Copy)
                    if u0 == 0:
                        act(T.m[:, 16 * H:16 * H + w], ps[4][:, 0:w], "", names("m1", 0, NS) + "b4", func=ACT.Relu)
                        for k in range(NS):
                            mm(ps[1][:, k:TK:16], T.m[:, H * (16 + k):H * (17 + k)], T.Wm[:, 16:32], False, False, "m1%d Wm" % k, "b1")
                    for k in range(u0, u1):
                        u_sum(1, k, T.ug[:, H * (16 + k):H * (17 + k)], "ug1%d" % k)
            if h == 0:
                for k in range(16):
                    u_sum(0, k, T.ug[:, k:16 * H:16] if i else T.ug[:, H * k:H * k + H], "ug0%d" % k)
        scan(0, 1)
        tt(T.Q[:, :], T.SC[:, 0:TK].indirect(T.oq[:, :]), T.CQ[:, :], MUL, "SC00 SC01 oq CQ", "Q")
        ts(T.W[:, 0:127], T.Q[:, 1:128], 8.0, MUL, "Q", "W")
        tt(T.A[:, :, 0:8], T.Q[:, :], T.W[:, :], SUB, "Q W W0", "Ad As0")
        tt(T.A[:, :, 7:11], T.A[:, :, 3:7], T.A[:, :, 3:7], MUL, "Ad", "As0")
        act(T.A[:, :, 11:15], T.A[:, :, 3:7], "Ad", "As1", func=ACT.Square)
        for b, h in ((2, 0), (3, 1), (3, 0)):
            mm(ps[b][:, H * h:H * h + H], T.A[:, 8 * h:8 * h + 8, :], T.I[:, :], True, True, "Ad As0 As1 Att I", "b%d" % b)
        ts(T.n2[:, :], T.Q[:, 0::8], -8192.0, MUL, "Q", "n2", 0.0, MAX)
        ts(T.n3[:, :], T.Q[:, 7::8], -4096.0, MUL, "Q", "n3")
        scan(1, 1)
        tt(T.n2[:, :], T.n2[:, :], T.n3[:, :], ADD, "n2 n3", "n2")
        ts(T.Rr[:, 0:H], ps[2][:, 0:H], col(cSR), MUL, "CC1", "R0 b2", col(cBR), ADD)
        act(T.Rr[:, H:TK], ps[3][:, H:TK], "CC1", "R1 b3", scale=col(cSR), bias=col(cBR))
        ts(T.L[:, 0:H], ps[2][:, 0:H], col(16), MUL, "CR", "L00 b2", col(17), ADD)
        act(T.L[:, TK:TK + H], ps[3][:, 0:H], "CR", "L01 b3", scale=col(18), bias=col(19))
        for gp in range(2):
            act(T.L[:, TK * gp + H:TK * gp + TK], ps[3][:, H:TK], "CR", "L1%d b3" % gp, scale=col(16 + 2 * gp), bias=col(17 + 2 * gp))
        for K in range(2):
            tt(T.X[:, 16 * K:16 * K + 16], T.n2[:, :], T.own[:, K, :], ADD, "n2 own", "X+")
        load(4, 0, (0,))
        load(5, 0, (2, 3))
        load(6, 0, (1,))
        load(7, 0, (4, 5))
        tt(T.po[:, :], T.SC[:, 15::16], T.X[:, :], ADD, "SC00 SC01 SC10 SC11 X", "po")
        reduce(4, 0, (0,))
        load(4, 0, (6, 7))
        reduce(6, 0, (1,))
        load(6, 1, (0, 1))
        reduce(5, 0, (2, 3))
        reduce(7, 0, (4, 5))
        load(7, 1, (2, 3))
        reduce(4, 0, (6, 7))
        reduce(6, 1, (0, 1))
        pools = HX + names("ca", 0, i + 1) + names("cb", 0, i + 1)
        lists = " Pl" + names("la", 0, i + 1) + names("lb", 0, i + 1)
        ids = "Pi" + names("D", 0, i + 1)
        e0 = TK * i

        def leave(h):
            a0 = TK * i + H * h
            cp(T.XS[:, a0:a0 + H], T.Pl[:, 0:c0 + TK].indirect(T.lx[:, 1, 8 * h:8 * h + 8]), "ix%d" % h + lists, "XS%d%d" % (i, h))
            send(dst, "arX%s%d" % ("ab"[h], i + 1), T.XR[:, a0 + TK:a0 + TK + H], T.XS[:, a0:a0 + H], "XS%d%d" % (i, h))

        def feats(h):
            a0 = TK * i + H * h
            act(T.CS[:, a0:a0 + H], T.Pf[:, 0:c0 + TK].indirect(T.lx[:, 1, 8 * h:8 * h + 8]), "ix%d" % h + pools, "CS%d%d" % (i, h), func=ACT.Copy)
            send(dst, "arc%s%d" % ("ab"[h], i + 1), T.Pf[:, c0 + TK + H * h:c0 + TK + H * h + H], T.CS[:, a0:a0 + H], "CS%d%d" % (i, h))

        load(5, 1, (6,))
        list_a(i, 0)
        reduce(5, 1, (6,))
        load(6, 1, (4, 5))
        load(4, 1, (7,))
        mm(ps[3][:, 0:TK], T.WB[:, 0:8, :], T.Rr[:, :], True, False, "WB0 R0 R1", "b3")
        mm(ps[3][:, 0:TK], T.WB[:, 8:16, :], T.Pi[:, c0:c0 + TK], False, True, "WB1 D%d" % i, "b3")
        list_b(0)
        if not last:
            leave(0)
        else:
            cp(T.IS[:, e0:e0 + H], T.Pi[:, 0:c0 + TK].indirect(T.lx[:, 1, 0:8]), "ix0 " + ids, "IS%d" % i)
            send(dst, "arF", T.Pi[:, c0 + TK:c0 + TK + H], T.IS[:, e0:e0 + H], "IS%d" % i)
        reduce(7, 1, (2, 3))
        if EARLY and not last:
            feats(0)
        reduce(4, 1, (7,))
        reduce(6, 1, (4, 5))
        list_a(i, 1)
        win, fi = T.U[:, 0:c0 + TK], T.lx[:, 0, :]

        def new_rows():
            act(T.B[:, :], ps[3][:, 0:TK], "CC1", "B b3", bias=col(cB0 + i))

        def lengths():
            for h in range(2):
                act(T.LN[:, i, 16 * i + h:16 * i + 16:2], T.YY[:, 24 * h:24 * h + 8], "y%d0 base" % h, "tk%d%d" % (i, h), func=ACT.Sign,
                    scale=-1.0, bias=T.base[:, 2 * i + h:2 * i + h + 1])
            args = (dst, "arN%d" % (i + 1), T.LN[:, i + 1, 0:16 * i + 16], T.LN[:, i, 0:16 * i + 16], "tk%d0 tk%d1 N%d" % (i, i, i))
            send(*args) if last else later.append(args)

        if not last:
            if not EARLY:
                feats(0)
            new_rows()
            lengths()
            list_b(1)
            act(T.Ag[:, :], win.indirect(fi), "U Ud ix0 ix1 CC1", "Ag", scale=col(cKEEP))
            leave(1)
            feats(1)
            tt(win.indirect(fi), T.Ag[:, :], T.B[:, :], ADD, "Ag B ix0 ix1", "U Ud")
            act(T.IS[:, e0:e0 + TK], T.Pi[:, 0:c0 + TK].indirect(T.lx[:, 1, :]), "ix0 ix1 " + ids, "IS%d" % i, func=ACT.Copy)
            later.append((dst, "arD%d" % (i + 1), T.Pi[:, c0 + TK:c0 + 2 * TK], T.IS[:, e0:e0 + TK], "IS%d C41" % i))
            turn_a(i + 1, 0)
            cp(T.On[:, :], T.XR[:, e0 + TK:e0 + TK + H], "Xa%d" % (i + 1), "On")
            turn_b(0)
        else:
            lengths()
            new_rows()
            list_b(1)
            act(T.IS[:, e0 + H:e0 + TK], T.Pi[:, 0:c0 + TK].indirect(T.lx[:, 1, 8:16]), "ix1 " + ids, "IT", func=ACT.Copy)
            send(dst, "arD%d" % R, T.Pi[:, c0 + TK + H:c0 + 2 * TK], T.IS[:, e0 + H:e0 + TK], "IT")
            cp(win.indirect(fi), T.B[:, :], "B ix0 ix1", "U Ud")

    dma("s", "o1", [(T.yh[:], T.U[RID::16, 0:V])], "U", "")
    c0 = V + TK * R
    for i in range(R):
        mm(ps[5][0:16, 0:H], T.LN[:, R, 16 * i:16 * i + 16], T.I[:, :], i == 0, i == R - 1, "I N%d" % R, "b5")
    mm(ps[4][0:8, 0:TK], T.Wo[:, :], T.Pi[:, c0:c0 + TK], True, True, "Wo F D%d" % R, "b4")
    act(T.Ft[0:8, :], ps[4][0:8, 0:TK], "", "Ft b4")
    ts(T.Fl[0:16, :], ps[5][0:16, 0:H], 0.5, MUL, "", "Fl b5", R / 2, ADD)
    dma("a", "o2", [(T.yt[:], T.Ft[0:8, :])], "Ft", "")
    dma("s", "o3", [(T.yl[:], T.Fl[0:16, :])], "Fl", "")
    for e in cnt:
        wait("g", ("s" + e, cnt[e], e, {}))
    wait("g", ("sent", sent[0], "g", {}))
    for s in final:
        wait("g", (s, final[s], "dma", {}))
